import numpy as np, ml_dtypes
CORES = [5,29,101,125,133,157,229,253]
N = 8
import mx_ref
BF = ml_dtypes.bfloat16
def gentries(a):
    return np.ascontiguousarray(a.reshape(8, 16, -1).transpose(0, 2, 1)).reshape(8, -1)
def gtable(e):
    e = np.asarray(e); return np.ascontiguousarray(e.reshape(8, -1, 16).transpose(0, 2, 1)).reshape(128, -1).astype(np.int32)
def gcols(t, e):
    v = np.concatenate([t.reshape(8, 16, -1, 4), np.zeros((8, 16, 1, 4), BF)], axis=2)
    return np.ascontiguousarray(np.stack([v[g][:, e[g]] for g in range(8)])).reshape(128, -1)
def tile(rs):
    return np.stack(rs, axis=2).reshape(128, -1).astype(BF)
def cut(t, i, w=512):
    return t[:, w * i:w * i + w]
def pick(q, e):
    c = np.concatenate([q[0].reshape(128, -1, 4), np.zeros((128, 1, 4), np.uint8)], axis=1); s = np.concatenate([q[1], np.ones((16, 1), np.uint8)], axis=1)
    return (np.ascontiguousarray(c[:, e].reshape(128, -1)), np.ascontiguousarray(s[:, e]))
def join(*qs):
    return (np.concatenate([q[0] for q in qs], axis=1), np.concatenate([q[1] for q in qs], axis=1))
def put(q, e, v):
    c, s = q[0].reshape(128, -1, 4).copy(), q[1].copy(); c[:, e] = v[0].reshape(128, -1, 4); s[:, e] = v[1]
    return (c.reshape(128, -1), s)
def pk(c, s):
    return (np.ascontiguousarray(c), mx_ref.live(s))
def emit(q):
    return q[0], q[1]
def packed(v, rng):
    q = [mx_ref.quantize(np.ascontiguousarray(v[r])) for r in range(N)]
    return np.stack([a for a, b in q]), np.stack([mx_ref.plane(b, rng) for a, b in q])
def values_of_codes():
    e, c = np.zeros((128, 128, 4), np.float32), np.zeros((128, 2, 4), np.uint8)
    e[np.arange(128), np.arange(128), 0] = 1
    c[:127, :, 0] = np.arange(256).reshape(2, 128).T[:127]
    return mx_ref.matmul(mx_ref.quantize(e.reshape(128, 512).astype(BF)), (c.reshape(128, 8), np.full((16, 2), 127, np.uint8))).T.reshape(-1).astype(np.float64)
CODE_VALUE, SCALE_VALUE = values_of_codes(), 2.0 ** (np.arange(256) - 127.0)
def decode(q):
    return (CODE_VALUE[q[0]].reshape(16, 8, -1, 4) * SCALE_VALUE[q[1]][:, None, :, None] + 0.0).reshape(128, -1).astype(np.float32)
def f(rng, *shape):
    return mx_ref.flush((rng.standard_normal(shape, dtype=np.float32) * np.exp2(rng.integers(-2, 3, shape[:-1] + (1,)))).astype(BF))
def wide(rng, *shape, cols=0):
    v = rng.standard_normal(shape, dtype=np.float32) * np.exp2(rng.integers(-12, 13, shape)).astype(np.float32)
    if cols: v *= np.repeat(np.exp2(rng.integers(-cols, cols + 1, shape[:-2] + (1, shape[-1] // 4))) * (rng.random(shape[:-2] + (1, shape[-1] // 4)) > 0.0625), 4, axis=-1).astype(np.float32)
    return mx_ref.flush(v.astype(BF))
C, K, R = 384, 160, 3
def trim(v):
    v = np.array(v, dtype=np.float32)
    v[np.abs(v) < np.float32(2.0 ** -16)] = 0
    return v.astype(BF)
def stored(t):
    return np.stack([gtable(e) for e in t])
def numbers_of(rng):
    return {"x": trim(f(rng, N, 128, 4 * C)), "tg": stored(rng.integers(0, C, (N, 8, C))), "u": np.array(f(rng, N, 128, 512)), "v": np.array(f(rng, N, 128, 512))}
def weights(rng, w):
    c, p = packed(w, rng)
    return {"wc": c, "ws": p}
def keeping(rng, n):
    w = trim(f(rng, N, 128, 2048)).reshape(N, 8, 16, 4, 8, 16, 4)
    w[:, :, :n] = 0
    w[:, :, :, :, :, :n] = 0
    w = w.reshape(N, 128, 4, 128, 4)
    i = np.flatnonzero(np.arange(128) % 16 < n)
    for b in range(4): w[:, i, b, i, b] = 32
    return weights(rng, w.reshape(N, 128, 2048))
def signs(rng):
    return np.stack([rng.permutation(8) % 2 * 2.0 - 1.0 for r in range(N)])
def sizes(rng):
    return np.where(rng.permutation(N) < N // 2, 2.0 ** -30, 1.0).astype(np.float32)
def marked(rng, fire, late, t):
    d = numbers_of(rng)
    k = sizes(rng)
    x = d["x"].astype(np.float32).reshape(N, 8, 16, C, 4)
    x[:, :, :8] = rng.integers(8, 14, (N, 8, 8, C, 4))
    x[:, :, 0, :, 0] = 8 + (fire > 0)
    x[:, :, 0, :, 1] = 8 + (fire < 0)
    x[:, :, 1, :, 0] = 8 + (late > 0)
    x[:, :, 1, :, 1] = 8 + (late < 0)
    x[:, :, :8] *= k[:, None, None, None, None]
    u = d["u"].reshape(N, 128, 128, 4)
    for h in range(0, 128, 16):
        for i in (h, h + 1):
            u[:, :, i] = 0
            u[:, i, i, 0] = k.astype(BF)
            u[:, i, i, 1] = (-k).astype(BF)
    return {"x": x.reshape(N, 128, 4 * C).astype(BF), "tg": stored(t), "u": u.reshape(N, 128, 512), "v": d["v"], **keeping(rng, 8)}
def setup_inputs(rng):
    return {**numbers_of(rng), **weights(rng, trim(f(rng, N, 128, 2048)))}
def setup_inputs_counts(rng):
    o = rng.permutation(N)
    fire = -rng.integers(0, 2, (N, 8, C))
    late = rng.integers(-1, 2, (N, 8, C))
    t = rng.integers(0, C, (N, 8, C))
    for r in range(N):
        n = rng.permutation([K, K, K - 1, K + 1, C, 1, 0, K // 2])
        if o[r] == 0: n[:] = 0
        if o[r] == 1: n[:] = C
        for g in range(8): fire[r, g, rng.permutation(C)[:n[g]]] = 1
        a = rng.permutation(8)
        late[r, a[0]] = 1
        late[r, a[1]] = 0
        t[r, a[2]] = rng.integers(C)
        t[r, a[3]] = np.arange(C)
        t[r, a[4]] = np.arange(C) // 2
    return marked(rng, fire, late, t)
def setup_inputs_waves(rng):
    n = min(K, C // 2) // 4 * 4
    h = n // 2
    p = np.argsort(rng.random((N, 8, C)), axis=2)
    i = np.arange(C)
    z = n + np.where(i < h, i // 2, np.where(i < n, i, h + (i - n) % h))
    fire = -rng.integers(0, 2, (N, 8, C))
    late = -rng.integers(0, 2, (N, 8, C))
    t = np.zeros((N, 8, C), np.int64)
    np.put_along_axis(t, p, np.roll(p, -1, axis=0)[:, :, z], axis=2)
    np.put_along_axis(fire, p[:, :, :n], 1, axis=2)
    np.put_along_axis(late, p[:, :, h:n], 1, axis=2)
    return marked(rng, fire, late, t)
def setup_inputs_near(rng):
    d = numbers_of(rng)
    p = rng.permutation(C)
    back = np.argsort(p)
    s = p // 2
    way = 1 - s % 2 * 2
    digit = ((s[:, None] >> np.arange(8)) & 1) * np.exp2(np.arange(8) - 22.0)
    x = np.zeros((N, 8, 16, C, 4), np.float32)
    x[:, :, 0, :, 0] = 1
    x[:, :, 8] = digit[:, :4]
    x[:, :, 9] = digit[:, 4:]
    x[:, :, 10:] = rng.integers(4, 8, (N, 8, 6, C, 4)) * rng.choice([-1.0, 1.0], (N, 8, 6, C, 4)) * 2.0 ** -19
    k, sign = sizes(rng), signs(rng)
    u = d["u"].reshape(N, 128, 128, 4)
    u[:, :, ::16] = 0
    u[:, :, 1::16] = 0
    t = rng.integers(0, C, (N, 8, C))
    for g in range(8):
        h = 16 * g
        a = (k * sign[:, g]).astype(np.float32).astype(BF)
        u[:, h, h, 0] = a
        u[:, h + 8:h + 10, h] = a[:, None, None]
        u[:, h + 10, h + 1] = k.astype(BF)[:, None]
    for r in range(N):
        a = rng.permutation(8)
        a = a[np.argsort(-sign[r, a], kind="stable")]
        for i in (0, 4):
            t[r, a[i]] = np.arange(C)
            t[r, a[i + 1]] = back[(p + way) % C]
            t[r, a[i + 2]] = back[(p - way) % C]
    return {"x": x.reshape(N, 128, 4 * C).astype(BF), "tg": stored(t), "u": u.reshape(N, 128, 512), "v": d["v"], **keeping(rng, 16)}
def setup_inputs_huge(rng):
    d = numbers_of(rng)
    o = rng.permutation(N)
    g = signs(rng)
    g[o == 0] = -1
    g[o == 1] = 1
    c = np.stack([rng.permutation(C) % 2 * 2.0 - 1.0 for r in range(N)])
    c[o < 3] = 1
    x = 2.0 ** 30 * (0.6 + 0.4 * rng.random((N, 128, C, 4))) * c[:, None, :, None]
    u = d["u"].reshape(N, 128, 128, 4)
    u[:, :, ::16] = (2.0 ** 30 * (1 - 0.25 * rng.random((N, 128, 8, 4))) * g[:, None, :, None]).astype(np.float32).astype(BF)
    return {"x": x.astype(np.float32).reshape(N, 128, 4 * C).astype(BF), "tg": d["tg"], "u": u.reshape(N, 128, 512), "v": d["v"], **keeping(rng, 16)}
def setup_inputs_spread(rng):
    d = setup_inputs(rng)
    d["x"] = trim(wide(rng, N, 128, 4 * C, cols=6))
    return d
def check_inputs(d):
    b = []
    for k in ("x", "u", "v"):
        a = np.abs(d[k].astype(np.float32))
        if not (np.isfinite(a).all() and ((a == 0) | (a >= 2.0 ** -30) & (a <= 2.0 ** 30)).all()): b.append("a value of " + k)
    if ((d["tg"] < 0) | (d["tg"] >= C)).any(): b.append("an entry of tg")
    for r in range(N):
        if ((d["wc"][r] & 127) == 127).any(): b.append("wc: a code that is no number")
        if not (np.abs(decode(pk(d["wc"][r], d["ws"][r]))) <= 2.0 ** 30).all(): b.append("a number of W")
    return b
def spreadout(m):
    return np.repeat(np.repeat(m, 16, axis=0), 4, axis=1)
def reference(x, tg, u, v, wc, ws):
    qu = [mx_ref.quantize(u[r]) for r in range(N)]
    lay = [pk(wc[r], ws[r]) for r in range(N)]
    to = [gentries(tg[r]).astype(np.int64) for r in range(N)]
    now = [x[r] for r in range(N)]
    last = [np.zeros((8, C), np.float32) for r in range(N)]
    fired = [np.zeros((8, C), bool) for r in range(N)]
    kept = [[] for r in range(N)]
    due = np.full((N, R + 2, 8, C), -1)
    lists = [None] * N
    for t in range(R + 1):
        if t > 0:
            for r in range(N):
                got = gcols(np.concatenate(kept[r], axis=1), due[r, t])
                mean = ((now[r].astype(np.float32) + got.astype(np.float32)) * np.float32(0.5)).astype(BF)
                now[r] = np.where(spreadout(due[r, t] >= 0), np.where(spreadout(fired[r]), mean, got), now[r])
        if t == R: break
        sent, target, delay = [], [], []
        for r in range(N):
            s = mx_ref.matmul(qu[r], mx_ref.quantize(now[r])) + np.float32(0.0)
            rise = s[::16] > last[r]
            last[r] = s[::16]
            e = np.argsort(~rise, axis=1, kind="stable")[:, :K]
            e = np.where(np.take_along_axis(rise, e, axis=1), e, -1)
            m = np.zeros((8, C + 1), bool)
            np.put_along_axis(m, np.where(e < 0, C, e), True, axis=1)
            fired[r] = m[:, :C]
            q = mx_ref.quantize(gcols(now[r], e))
            h = tile([np.maximum(mx_ref.matmul(pick(lay[r], np.arange(128 * b, 128 * b + 128)), q), np.float32(0.0)) * np.float32(0.03125) for b in range(4)])
            sent.append(mx_ref.quantize(h))
            some = np.maximum(e, 0)
            target.append(np.take_along_axis(to[r], some, axis=1))
            delay.append(np.where(e < 0, 0, 1 + (np.take_along_axis(s[1::16], some, axis=1) > 0)))
            lists[r] = e
        came = decode(join(*sent)).astype(BF)
        for r in range(N):
            n = (r + 1) % N
            kept[n].append(cut(came, r, 4 * K))
            for w in (1, 2):
                for g in range(8):
                    k = np.flatnonzero(delay[r][g] == w)[::-1]
                    new = np.full(C, -1)
                    new[target[r][g, k]] = K * t + k
                    due[n, t + w, g] = np.where(due[n, t + w, g] < 0, new, due[n, t + w, g])
    y, ol = np.zeros((N, 128, C), np.float32), np.zeros((N, 8, K), np.float32)
    oc, osc = np.zeros((N, 128, 4 * C), np.uint8), np.zeros((N, 16, C), np.uint8)
    for r in range(N):
        q = mx_ref.quantize(now[r])
        y[r] = mx_ref.matmul(mx_ref.quantize(v[r]), q)
        ol[r] = lists[r]
        oc[r], osc[r] = emit(q)
    return {"y": y, "ol": ol, "oc": oc, "osc": osc}

@@ -1,0 +1,575 @@
+from concourse.bass import DstId, RemoteDMATransfer
+from concourse.mybir import dt, AluOpType as A, ActivationFunctionType as F
+
+C, K, N = 384, 160, 8
+HALF = K // 2
+CV = C + 15
+CS = C + 32
+MID = 208
+NZ = 4 * C + 4
+M1, V1, WEND = 400, 560, 1360
+LT = 10
+STEP = 2.0 ** -11
+R1 = 1.5 * 2.0 ** 23
+F32, BF, I32, U16, COD, U8 = "float32", "bfloat16", "int32", "uint16", "float8_e4m3fn_x4", "uint8"
+SCRATCH = {}
+
+
+def _b(name, n, d, where="sbuf"):
+    SCRATCH[name] = (where, [128, n], d)
+
+
+for _t in range(4):
+    _b("XT%d" % _t, 4 * C, BF)
+    _b("xq%d" % _t, C, COD)
+    _b("xs%d" % _t, C, U8)
+    _b("ebq%d" % _t, 128, COD)
+    _b("ebs%d" % _t, 128, U8)
+    _b("XG%d" % _t, K, BF)
+    _b("XD%d" % _t, K, BF)
+    _b("WB%d" % _t, WEND, BF)
+for _t in range(3):
+    for _n, _w, _d in [("hq", K, COD), ("hs", K, U8), ("hl", K, COD), ("hls", K, U8), ("tm", LT, U16), ("wm", 64, BF),
+                       ("lt", LT, U16), ("lw", 64, BF), ("rc", HALF, COD), ("rs", K, U8), ("rt", LT, U16), ("rw", 64, BF)]:
+        _b("%s%d" % (_n, _t), _w, _d)
+for _n, _w, _d in [
+        ("UT", 512, BF), ("VT", 512, BF), ("uq", 128, COD), ("us", 128, U8), ("ur", 128, COD), ("urs", 128, U8),
+        ("ul", 128, COD), ("uls", 128, U8), ("vq", 128, COD), ("vs", 128, U8), ("wq", 512, COD), ("wsp", 512, U8),
+        ("tgT", 24, I32), ("RW", 2 * C, BF), ("tg2s", 48, BF), ("tl", 24, I32), ("lanep", 1, I32), ("lanei", 1, I32), ("half", 516, BF),
+        ("EBW", 516, BF), ("vi", 24, I32), ("ET", 4 * K, BF), ("eq", K, COD), ("es", K, U8), ("HT", 4 * K, BF), ("OLr", K, F32),
+        ("YT", C, F32)]:
+    _b(_n, _w, _d)
+PLACE, _end = {}, {}
+for _n, _w, _d in [
+        ("lane", 1, F32), ("lane48", 1, F32), ("vini", 1, F32), ("thr", 1, F32), ("sc", 1, F32), ("scA", 1, F32), ("m16", 24, F32),
+        ("m24", 24, F32), ("x36", 36, F32), ("xf", 36, F32), ("q1", 36, F32), ("fl", 36, F32), ("q2", 36, F32), ("q3", 36, F32),
+        ("q4", 36, F32), ("q5", 36, F32), ("q6", 36, F32), ("RL", 36, U16), ("PL", 36, U16), ("KC", 576, BF), ("i16", CS, BF),
+        ("iota4", C, F32), ("xio", C, F32), ("IOTA", 400, F32), ("iotaj", 400, F32), ("mt16", 16, F32), ("D2", CS, BF), ("own", 16, BF),
+        ("hlf", 16, BF), ("pw", 16, F32), ("nr24", 576, BF), ("nr16", 32, F32), ("ones32", 32, F32), ("lu", 8, U16), ("ll", 8, U16),
+        ("nT", 24, F32), ("posl", 24, U16), ("posm", 24, U16), ("zr", 416, BF), ("ngc", 400, BF),
+        ("cT", 24, F32), ("OH", 576, BF), ("C1", 576, BF), ("Hh", 32, F32), ("HT1", 32, F32), ("PI", 32, F32), ("G1", 64, F32),
+        ("GT", 64, F32), ("BI", 33, F32), ("G2", 24, F32), ("C2", 576, BF), ("C2m", 576, BF), ("NOm", 576, BF),
+        ("SEL", 576, BF), ("rk", 24, U16), ("pir", CS, F32), ("pis", CS, F32), ("pi4", 26, U16), ("bx", 32, F32), ("be", 32, F32),
+        ("endl", 2, U16), ("tgx", 400, F32), ("LMr", C, BF), ("NS", CS, BF), ("ZS0", CS, BF),
+        ("P0", 1600, BF), ("P1", 1600, BF), ("Z", 1600, BF), ("RQ", 400, BF), ("PS", 400, F32),
+        ("ac1", 1, F32), ("al", 1, U16), ("TA", 16, F32), ("FF", 17, F32), ("FD", 16, F32), ("el", 10, U16),
+        ("ZS", CS, BF), ("SD1", CS + 1, BF), ("SD2", CS + 1, BF), ("LAST", C, F32), ("junk1", 400, BF),
+        ("TT", K, F32), ("TS", K, F32), ("FX", C, F32), ("FS", C, F32), ("fl24", 24, F32), ("fvV", 24, F32),
+        ("RR", 24, F32), ("h1", 24, F32), ("d1", 24, F32), ("p1", 24, F32), ("h2", 24, F32), ("e0", 24, F32),
+        ("e1", 24, F32), ("p2", 24, F32), ("h3", 24, F32), ("qf", 24, F32), ("fin", 24, U16)]:
+    PLACE[_n] = ("pack_" + _d, _end.get(_d, 0), _w)
+    _end[_d] = _end.get(_d, 0) + (_w + 31) // 32 * 32
+SCRATCH["tg2"] = ("dram", [128, 48], BF)
+for _d in _end:
+    _b("pack_" + _d, _end[_d], _d)
+PSUM = ["pw0", "pw1", "pw2", "pw3", "psr", "psl", "py", "py2"]
+for _n in PSUM:
+    _b(_n, 512, F32, "psum")
+
+SEMAPHORES = (["cv", "cs", "ct", "cg", "dx", "du", "dtg", "dtr", "drw", "dwc", "dws", "dv", "dol", "doc0", "doc1", "dos", "dy0", "dy1", "ls", "ro"]
+              + ["%s%d" % (_s, _t) for _s in ("la", "lb", "lm", "ha", "rl", "rb", "rm", "rh") for _t in range(3)])
+
+
+def _bits(es):
+    return sum(1 << e for e in es)
+
+
+def _relays(rank, T, topo):
+    me, dst = T.cores[rank], T.cores[(rank + 1) % N]
+    able = [c for c in topo.cores_of(me) if c != me and topo.may_write(c, dst)]
+    near = [c for c in able if topo.die(c) == topo.die(me)]
+    far = [c for c in able if topo.die(c) != topo.die(me)]
+    return near[0], far[0], near[1], far[1]
+
+
+def _relay_program(g, core, role, src, dst, T, topo):
+    rid, pid = topo.addr(dst, core)
+    mask, n_out, n_all = topo.mask(core, dst), len(topo.engines(core, dst)), len(topo.engines(src, core))
+    sent = [0]
+
+    def fwd(out, in_, sem):
+        g.remote_dma(out, in_, T.sem[sem], T.sem.ro, pid, rid, mask)
+        sent[0] += n_out
+
+    for t in range(3):
+        if role == 3:
+            g.wait_ge(T.sem["rb%d" % t], n_all)
+            fwd(T["lt%d" % t][:, 0:LT], T["rt%d" % t][:, 0:LT], "lb%d" % t)
+            for at, a, b in ((0, "rl", "la"), (32, "rm", "lm"))[:2 if t < 2 else 1]:
+                g.wait_ge(T.sem["%s%d" % (a, t)], n_all)
+                fwd(T["lw%d" % t][:, at:at + 32], T["rw%d" % t][:, at:at + 32], "%s%d" % (b, t))
+        elif role == 2:
+            g.wait_ge(T.sem["rh%d" % t], n_all)
+            fwd(T["hls%d" % t][:, 0:K], T["rs%d" % t][:, 0:K], "ha%d" % t)
+        else:
+            g.wait_ge(T.sem["rh%d" % t], n_all // 2)
+            fwd(T["hl%d" % t][:, HALF * role:HALF * role + HALF].bitcast(dt.uint8), T["rc%d" % t][:, 0:HALF].bitcast(dt.uint8), "ha%d" % t)
+    g.wait_ge(T.sem.ro, sent[0])
+
+
+def rank_program(g, core, T, topo):
+    rank = T.rank_of(core)
+    if rank is None:
+        for r, c in enumerate(T.cores):
+            if core in topo.cores_of(c):
+                rel = _relays(r, T, topo)
+                if core in rel:
+                    _relay_program(g, core, rel.index(core), c, T.cores[(r + 1) % N], T, topo)
+        return
+    queue = {"v": g.vector, "s": g.scalar, "t": g.tensor, "g": g, "y": g.sync}
+    own = {"v": "cv", "s": "cs", "t": "ct", "g": "cg"}
+    total, waited, known = {}, {}, {q: {} for q in queue}
+    writer, readers = {}, {}
+
+    def deps(q, R, W):
+        evs = [writer[k] for k in R if k in writer]
+        for k in W:
+            evs += readers.get(k, []) + ([writer[k]] if k in writer else [])
+        for e in sorted(evs, key=lambda e: (-sum(e["clock"].values()), e["sem"])):
+            if known[q].get(e["sem"], 0) < e["n"]:
+                queue[q].wait_ge(T.sem[e["sem"]], e["n"])
+                waited[e["sem"]] = max(waited.get(e["sem"], 0), e["n"])
+                for s, n in e["clock"].items():
+                    known[q][s] = max(known[q].get(s, 0), n)
+
+    def note(sem, kq, R, W):
+        clock = dict(known[kq]) if kq else {}
+        clock[sem] = total[sem]
+        ev = {"sem": sem, "n": total[sem], "clock": clock}
+        for k in R:
+            readers.setdefault(k, []).append(ev)
+        for k in W:
+            writer[k], readers[k] = ev, []
+
+    def p(name, a=0, b=None, step=1, key=None):
+        buf, at, w = PLACE[name] if name in PLACE else (name, 0, SCRATCH[name][1][1])
+        return T[buf][:, at + a:at + (w if b is None else b):step], [name] if key is None else [key] if isinstance(key, str) else list(key)
+
+    def ix(win, off):
+        return win[0].indirect(off[0]), win[1] + off[1]
+
+    def cast(x, d):
+        return x[0].bitcast(d), x[1]
+
+    def op(q, fn, outs, ins):
+        R = sorted({k for o in ins for k in o[1]})
+        W = sorted({k for o in outs for k in o[1]} | {k for k in R if k in PSUM})
+        deps(q, R, W)
+        total[own[q]] = total.get(own[q], 0) + 1
+        fn().then_inc(T.sem[own[q]], 1)
+        note(own[q], q, R, W)
+
+    def dma(q, pairs, sem, R, W):
+        deps(q, R, W)
+        for o, i in pairs:
+            queue[q].dma_start(o, i).then_inc(T.sem[sem], 16)
+            total[sem] = total.get(sem, 0) + 16
+        note(sem, q, R, W)
+
+    v, s = g.vector, g.scalar
+
+    def val(x):
+        return x[0] if isinstance(x, tuple) else x
+
+    def ts(out, in0, a, o0, b=None, o1=None):
+        ins = [in0] + [x for x in (a, b) if isinstance(x, tuple)]
+        if o1 is None:
+            op("v", lambda: v.tensor_scalar(out[0], in0[0], val(a), None, o0), [out], ins)
+        else:
+            op("v", lambda: v.tensor_scalar(out[0], in0[0], val(a), val(b), o0, o1), [out], ins)
+
+    def tt(out, a, b, o):
+        op("v", lambda: v.tensor_tensor(out[0], a[0], b[0], o), [out], [a, b])
+
+    def cp(out, in_):
+        op("v", lambda: v.tensor_copy(out[0], in_[0]), [out], [in_])
+
+    def fill(out, c):
+        op("v", lambda: v.memset(out[0], c), [out], [])
+
+    def scan(out, d0, d1, init, o0, o1):
+        op("v", lambda: v.tensor_tensor_scan(out[0], d0[0], d1[0], val(init), o0, o1), [out], [d0, d1] + ([init] if isinstance(init, tuple) else []))
+
+    def turn(out, in_):
+        op("v", lambda: v.transpose(out[0], in_[0]), [out], [in_])
+
+    def act(out, in_, func=F.Copy, **kw):
+        op("s", lambda: s.activation(out[0], in_[0], func, **kw), [out], [in_])
+
+    def signs(junk, in_, bias, accum):
+        op("s", lambda: s.activation(junk[0], in_[0], F.Sign, bias=bias[0], accum_out=accum[0], scale=-1.0), [junk, accum], [in_, bias])
+
+    def copy(q, out, in_):
+        (cp if q == "v" else act)(out, in_)
+
+    def quant(c, sc, in_):
+        op("v", lambda: v.quantize_mx(c[0], sc[0], in_[0]), [c, sc], [in_])
+
+    def mm(out, l, ls, r, rs):
+        op("t", lambda: g.tensor.matmul_mx(out[0], l[0], ls[0], r[0], rs[0], True, True), [out], [l, ls, r, rs])
+
+    def iota(out, pattern, base=0, ch=0):
+        op("g", lambda: g.iota(out[0], pattern, base, ch, allow_small_or_imprecise_dtypes=True), [out], [])
+
+    def lane_scan(out, row, n):
+        scan(out, p("D2", 0, n), row, 0.0, A.mult, A.max)
+
+    def unlane(out, rows, off=0.0):
+        ts(out, rows, p("scA"), A.mult, -2048.0 - off, A.add)
+
+    def XT(t, b=None):
+        return p("XT%d" % t, 0, 4 * C, 1, ["XT%d_%d" % (t, i) for i in range(4)]) if b is None else p("XT%d" % t, b, 4 * C, 4, "XT%d_%d" % (t, b))
+
+    def WB(b, a, e, parts):
+        return p("WB%d" % b, a, e, 1, ["W%s_%d" % (k, b) for k in parts])
+
+    dma("s", [(T.XT0[:, 0:4 * C], T.x[:, :])], "dx", [], XT(0)[1])
+    dma("y", [(T.tgT[:, :], T.tg[:, :])], "dtg", [], ["tgT"])
+    dma("y", [(T.UT[:, :], T.u[:, :])], "du", [], ["UT"])
+    dma("y", [(T.wq[:, :].bitcast(dt.uint8), T.wc[:, :])], "dwc", [], ["wq"])
+    dma("y", [(T.wsp[:, :], T.ws[:, :])], "dws", [], ["wsp"])
+    dma("y", [(T.VT[:, :], T.v[:, :])], "dv", [], ["VT"])
+
+    fill(p("half"), 0.5)
+    iota(p("lanep"), [[1, 1]], 0, 1)
+    iota(p("x36"), [[16, 36]])
+    iota(p("m16"), [[16, 24]])
+    iota(p("KC"), [[1, 24], [0, 24]])
+    iota(p("m24"), [[1, 24]])
+    iota(p("i16"), [[0, 26], [1, 16]])
+    iota(p("mt16"), [[16, 16]], -64)
+    iota(p("IOTA"), [[1, 400]])
+    for b in range(4):
+        iota(WB(b, C, M1, "0"), [[0, 16]])
+    op("g", lambda: g.affine_select(T.EBW[:, :], T.half[:, :], [[1, 516]], A.is_equal, 0.0, -3, -4), [p("EBW")], [p("half")])
+    iota(p("NS"), [[0, CS]], 1)
+    iota(p("ZS0"), [[0, CS]])
+    iota(p("iota4"), [[4, C]], 3)
+    iota(p("iotaj", 0, C), [[1, C]])
+    iota(p("iotaj", C, 400, 1, "iotajp"), [[0, 16]], -1)
+
+    ts(p("lanei"), p("lanep"), 15, A.bitwise_and)
+    fill(p("Hh"), 0.0)
+    cp(p("lane"), p("lanei"))
+    fill(p("ones32"), 1.0)
+    ts(p("xf"), p("x36"), p("lane"), A.add)
+    fill(p("hlf"), 0.5)
+    fill(p("nr24"), 1.0)
+    fill(p("BI", 0, 1, 1, "BI0"), -1.0 - MID)
+    fill(p("P0", 4 * C + 2, 4 * C + 4, 1, "P0z"), 0.0)
+    ts(p("P0", 4 * C + 1, 4 * CV, 4, "P0v"), p("hlf", 0, 15), 2.0, A.mult)
+    ts(p("q1"), p("xf"), 1.0 / 24, A.mult, -11.5 / 24, A.add)
+    ts(p("q3"), p("xf"), -24.0, A.mult, 552.0, A.add)
+    ts(p("fl"), p("q1"), R1, A.add, R1, A.subtract)
+    ts(p("q2"), p("fl"), -24.0, A.mult)
+    ts(p("q4"), p("fl"), 577.0, A.mult)
+    tt(p("q5"), p("q2"), p("xf"), A.add)
+    tt(p("q6"), p("q4"), p("q3"), A.add)
+    cp(p("RL"), p("q5"))
+    cp(p("PL"), p("q6"))
+    ts(p("tl"), p("tgT"), 15, A.bitwise_and)
+    ts(p("tg2s", 0, 24, 1, "tg2a"), p("tgT"), -192.0, A.add)
+    cp(p("tg2s", 24, 48, 1, "tg2b"), p("tl"))
+    dma("y", [(T.tg2[:, :], T.tg2s[:, :])], "dtr", ["tg2a", "tg2b"], ["tg2"])
+    dma("y", [(T.RW[i:128:16, :], T.tg2[:, :]) for i in range(16)], "drw", ["tg2"], ["RW"])
+    ts(p("vi"), p("tgT"), 4, A.arith_shift_right)
+    tt(p("OH"), ix(p("vi"), p("RL")), p("KC"), A.is_equal)
+    ts(p("nr24", 0, 576, 24), p("nr24", 0, 576, 24), 0.0, A.mult)
+    scan(p("C1"), p("nr24"), p("OH"), 0.0, A.mult, A.add)
+    cp(p("Hh", 0, 24), p("C1", 23, 576, 24))
+    turn(p("HT1"), p("Hh"))
+    cp(p("lu"), p("m16", 0, 8))
+    quant(p("uq"), p("us"), p("UT"))
+    cp(cast(p("ur"), dt.uint32), ix(cast(p("uq"), dt.uint32), p("lu")))
+    for i in range(3):
+        act(p("P1", 516 * i, min(516 * i + 516, NZ), 1, "P1"), p("half", 0, min(516, NZ - 516 * i)), scale=0.0)
+    act(p("P0", 0, NZ, 4, "P0"), p("half", 0, C + 1), scale=0.0)
+    act(p("ngc"), p("half", 0, 400), F.Identity, scale=0.0, bias=-2064.0 - 80.0)
+    act(p("zr"), p("half", 0, 416), scale=0.0)
+    act(p("NOm"), ix(p("OH"), p("PL")), scale=-1000.0)
+    act(p("urs"), ix(p("us"), p("lu")))
+
+    def quant_x(t):
+        quant(p("xq%d" % t), p("xs%d" % t), XT(t))
+
+    def planes(t, q, bs):
+        for b in bs:
+            copy(q, WB(b, 0, C, "X"), XT(t, b))
+
+    def scores(t):
+        mm(p("psr", 0, C), p("ur"), p("urs"), p("xq%d" % t), p("xs%d" % t))
+
+    def scores_late(t):
+        mm(p("psl", 0, C), p("ul"), p("uls"), p("xq%d" % t), p("xs%d" % t))
+
+    def rise(t):
+        tt(p("P0", 1, 4 * C, 4, "P0r"), p("psr", 0, C), p("LAST"), A.is_gt)
+
+    def entries():
+        flags = p("P0", 1, 4 * CV, 4, ["P0", "P0r", "P0v"])
+        scan(p("P1", 0, 4 * CV, 4, "P1y"), flags, (p("zr", 0, CV)[0], ["zr", "P1"]), -161.0, A.add, A.min)
+        signs(p("junk1", 0, CV), p("P1", 0, 4 * CV, 4, "P1y"), p("thr"), p("ac1"))
+        scan(p("RQ", 0, CV), flags, p("zr", 0, CV), p("vini"), A.add, A.add)
+        scan(p("PS", 1, 1 + CV), p("RQ", 0, CV), p("ngc", 0, CV), 0.0, A.add, A.add)
+
+    def runs_end():
+        ts(p("al"), p("ac1"), float(CV), A.add, 0.5, A.mult)
+        tt(p("TA"), ix(p("IOTA"), p("al")), p("mt16"), A.mult)
+        tt(p("FF", 1, 17), ix(p("PS", 0, 400, 1, ["PS", "PS0"]), p("al")), p("TA"), A.subtract)
+        tt(p("FD"), p("FF", 0, 16, 1, ["FF", "FF0"]), p("FF", 1, 17), A.subtract)
+        ts(p("el"), p("FD", 0, 10), 1.0 / 16, A.mult)
+
+    def late(t):
+        o = p("P0", 2, 4 * C, 4, "P0l")
+        op("s", lambda: s.activation(o[0], p("psl", 0, C)[0], F.Sign, bias=-2.0 ** -118), [o], [p("psl")])
+
+    def signed():
+        scan(p("Z", 0, NZ), p("P0", 0, NZ, 1, ["P0", "P0r", "P0v", "P0l", "P0m", "P0z"]), p("P1", 0, NZ, 1, ["P1", "P1y"]), 0.0, A.mult, A.add)
+
+    def resolve(t):
+        if t == 0:
+            cp(ix(p("ZS0"), p("rk")), p("Z", 3, 4 * C, 4))
+        else:
+            cp(p("ZS"), ix(p("Z", 0, NZ), p("pi4")))
+        scan(p("SD1", 1, CS + 1), p("NS"), p("ZS" if t else "ZS0"), 0.0, A.mult, A.max)
+        act(p("wm%d" % t, 0, 32, 1, "wm%da" % t), ix(p("SD1", 0, CS, 1, ["SD1", "SD10"]), p("endl")))
+        send_winners(t, "a", 0, "rl")
+
+    def resolve_late(t):
+        act(p("FX"), p("Z", 1, 4 * C, 4), F.Identity, scale=-(2.0 ** -8), bias=1.0)
+        if t < 2:
+            scan(p("SD2", 1, CS + 1), p("NS"), p("ZS" if t else "ZS0"), 0.0, A.mult, A.min)
+            act(p("wm%d" % t, 32, 64, 1, "wm%db" % t), ix(p("SD2", 0, CS, 1, ["SD2", "SD20"]), p("endl")), scale=-1.0)
+            send_winners(t, "b", 32, "rm")
+
+    def gather_e(t, pairs):
+        for b, q in pairs:
+            copy(q, p("ET", b, None, 4, "ET%d" % b), ix(WB(b, 0, M1, "X0"), p("el")))
+
+    def layer(t):
+        quant(p("eq"), p("es"), p("ET", 0, None, 1, ["ET%d" % b for b in range(4)]))
+        for b in range(4):
+            mm(p("pw%d" % b, 0, K), p("wq", 128 * b, 128 * b + 128), p("wsp", 128 * b, 128 * b + 128), p("eq"), p("es"))
+
+    def targets_row():
+        act(p("TT"), ix(p("tgx", 0, 400, 1, ["tgx", "tgxp"]), p("el")))
+
+    def targets(t):
+        lane_scan(p("TS"), p("TT"), K)
+        unlane(p("tm%d" % t), p("TS", 15, K, 16))
+
+    def relus(pairs):
+        for b, q in pairs:
+            o, i = p("HT", b, None, 4, "HT%d" % b), p("pw%d" % b, 0, K)
+            if q == "s":
+                act(o, i, F.Relu, scale=0.03125)
+            else:
+                ts(o, i, 0.0, A.max, 0.03125, A.mult)
+
+    def quant_h(t):
+        quant(p("hq%d" % t), p("hs%d" % t), p("HT", 0, None, 1, ["HT%d" % b for b in range(4)]))
+
+    rel = _relays(rank, T, topo)
+
+    def send(i, out, in_, sem):
+        rid, pid = topo.addr(rel[i], core)
+        g.remote_dma(out, in_, T.sem[sem], T.sem.ls, pid, rid, topo.mask(core, rel[i]))
+        total["ls"] = total.get("ls", 0) + len(topo.engines(core, rel[i]))
+
+    def send_codes(t):
+        deps("g", ["hq%d" % t, "hs%d" % t], [])
+        es = topo.engines(core, rel[0])
+        h, tr = len(es) // 2, []
+        for i in range(2):
+            rid, pid = topo.addr(rel[i], core)
+            tr.append(RemoteDMATransfer(dst_ids=[DstId(rid=rid, pnc=pid)], dma_engine_mask=_bits(es[h * i:h * i + h]), remote_sem=T.sem["rh%d" % t],
+                                        src=T["hq%d" % t][:, HALF * i:HALF * i + HALF].bitcast(dt.uint8), dst=T["rc%d" % t][:, 0:HALF].bitcast(dt.uint8)))
+        g.remote_dma_fused(tr, local_sem=T.sem.ls)
+        total["ls"] = total.get("ls", 0) + 2 * h
+        send(2, T["rs%d" % t][:, 0:K], T["hs%d" % t][:, 0:K], "rh%d" % t)
+
+    def send_targets(t):
+        deps("g", ["tm%d" % t], [])
+        send(3, T["rt%d" % t][:, 0:LT], T["tm%d" % t][:, 0:LT], "rb%d" % t)
+
+    def send_winners(t, k, at, sem):
+        deps("g", ["wm%d%s" % (t, k)], [])
+        send(3, T["rw%d" % t][:, at:at + 32], T["wm%d" % t][:, at:at + 32], "%s%d" % (sem, t))
+
+    def between(t):
+        n = t + 1
+        if t < 2:
+            act(p("LAST"), p("psr", 0, C))
+        if n >= 2:
+            for b in range(4):
+                tt(WB(b, V1 + 320 * (t - 1), V1 + 320 * (t - 1) + K, ["A%d" % (t - 1)]), p("pw%d" % b, 0, K), p("XD%d" % b), A.add)
+        lane_scan(p("FS"), p("FX"), C)
+        ts(p("fl24"), p("FS", 15, C, 16), p("sc"), A.mult, 1.0, A.is_gt)
+        ts(p("fvV"), p("fl24"), 160.0, A.mult, float(V1 + 320 * t), A.add)
+        if n >= 2:
+            older = p("lw%d" % (t - 1), 32, 56, 1, "lx%d" % (t - 1))
+            ts(p("h2"), older, 0.0, A.is_gt)
+            ts(p("e0"), older, -1.0, A.mult, -320.0, A.add)
+            tt(p("e1"), p("e0"), p("fvV"), A.add)
+            tt(p("p2"), p("e1"), p("h2"), A.mult)
+            tt(p("RR"), p("p2"), p("cT"), A.max)
+            ts(p("h3"), p("h2"), -8192.0, A.mult)
+            tt(p("fvV"), p("fvV"), p("h3"), A.add)
+
+    def older_unpacked(t):
+        for b in range(4):
+            act(p("XD%d" % b), ix(WB(b, 0, M1, ["X", "0"]), p("lt%d" % (t - 1))), scale=0.5)
+        for b in range(4):
+            mm(p("pw%d" % b, 0, K), p("ebq%d" % b), p("ebs%d" % b), p("hl%d" % (t - 1)), p("hls%d" % (t - 1)))
+
+    def merge(n):
+        t = n - 1
+        lw, lt, m, a = "lw%d" % t, "lt%d" % t, M1 + 320 * t, V1 + 320 * t
+        for b, q in ((0, "s"), (3, "v"), (1, "s"), (2, "s")):
+            o, i = p("XG%d" % b), ix(WB(b, 0, M1, ["X", "0"]), p(lt))
+            if q == "s":
+                act(o, i, scale=0.5)
+            else:
+                ts(o, i, 0.5, A.mult)
+        for b in range(4):
+            mm(p("pw%d" % b, 0, K), p("ebq%d" % b), p("ebs%d" % b), p("hl%d" % t), p("hls%d" % t))
+
+        def mean(b):
+            tt(WB(b, a, a + K, ["A%d" % t]), p("pw%d" % b, 0, K), p("XG%d" % b), A.add)
+
+        def move(b):
+            act(WB(b, m, m + K, ["M%d" % t]), p("pw%d" % b, 0, K), scale=2.0)
+
+        def final():
+            ts(p("h1"), p(lw, 0, 24), 0.0, A.is_gt)
+            tt(p("d1"), p("fvV"), p(lw, 0, 24), A.subtract)
+            tt(p("p1"), p("d1"), p("h1"), A.mult)
+            tt(p("qf"), p("p1"), p("cT" if n == 1 else "RR"), A.max)
+            cp(p("fin"), p("qf"))
+
+        mean(0), move(1), mean(2), move(3), mean(1), move(0)
+        final()
+        mean(3), move(2)
+        for b, q in ((0, "v"), (1, "s"), (2, "v"), (3, "s")):
+            copy(q, XT(n, b), ix(WB(b, 0, a + K, ["X", "0"] + ["%s%d" % (k, i) for i in range(n) for k in "MA"]), p("fin")))
+
+    for t in range(3):
+        for sem, n, keys in (("lb", 8, ["lt%d" % t]), ("la", 8, ["lw%d" % t]), ("lm", 8, ["lx%d" % t]), ("ha", 24, ["hl%d" % t, "hls%d" % t])):
+            if sem == "lm" and t == 2:
+                continue
+            total["%s%d" % (sem, t)] = n
+            note("%s%d" % (sem, t), None, [], keys)
+
+    quant_x(0)
+    scores(0)
+    ts(p("nr16"), p("i16", 0, 32), 0.0, A.is_gt)
+    scan(p("PI"), p("nr16"), p("HT1"), 0.0, A.mult, A.add)
+    tt(p("G1", 0, 32), p("PI"), p("HT1"), A.subtract)
+    for a in range(2):
+        ts(p("G1", 32 + 16 * a, 48 + 16 * a, 1, "G1%d" % a), p("ones32", 0, 16), p("PI", 16 * a + 15, 16 * a + 16), A.mult, 1.0, A.add)
+    turn(p("GT"), p("G1", key=["G1", "G10", "G11"]))
+    scan(p("BI", 1, 33), p("ones32"), p("GT", 32, 64), -1.0 - MID, A.mult, A.add)
+    tt(p("G2"), p("GT", 0, 24), p("BI", 0, 24, 1, ["BI", "BI0"]), A.add)
+    tt(p("OH", 0, 576, 24), p("OH", 0, 576, 24), p("G2"), A.add)
+    scan(p("C2"), p("nr24"), p("OH"), 0.0, A.mult, A.add)
+    planes(0, "s", (0, 1))
+    act(p("C2m"), ix(p("C2"), p("PL")))
+    ts(p("ll"), p("m16", 0, 8), 1.0, A.add)
+    ts(p("vini"), p("lane"), -1.0, A.mult, 2064.0 + 7.5, A.add)
+    ts(p("thr"), p("lane"), 16.0, A.mult, -145.5, A.add)
+    fill(p("PS", 0, 1, 1, "PS0"), 0.0)
+    fill(p("FF", 0, 1, 1, "FF0"), 0.0)
+    fill(p("tgx", C, 400, 1, "tgxp"), 1.0)
+    ts(p("P0", 1, 4 * C, 4, "P0r"), p("psr", 0, C), 0.0, A.is_gt)
+    entries()
+    runs_end()
+    planes(0, "s", (2, 3))
+    scan(p("SEL"), p("NOm"), p("C2m"), -2000.0, A.add, A.max)
+    cp(cast(p("ul"), dt.uint32), ix(cast(p("uq"), dt.uint32), p("ll")))
+    ts(p("lane48"), p("lane"), 48.0, A.mult)
+    ts(p("nT"), p("m24"), p("lane48"), A.add)
+    ts(p("posm"), p("nT"), 24.0, A.add)
+    cp(p("posl"), p("nT"))
+    gather_e(0, ((0, "s"), (2, "v"), (1, "s"), (3, "v")))
+    layer(0)
+    act(p("uls"), ix(p("us"), p("ll")))
+    scores_late(0)
+    ts(p("rk"), p("SEL", 23, 576, 24), float(MID), A.add)
+    ts(p("D2"), p("i16"), p("lane"), A.not_equal, 2.0, A.mult)
+    ts(p("own"), p("i16", 0, 16), p("lane"), A.is_equal)
+    scan(p("pw"), p("hlf"), p("own"), 0.0, A.mult, A.max)
+    cp(p("sc"), p("pw", 15, 16))
+    ts(p("scA"), p("sc"), 2048.0, A.mult)
+    ts(p("bx"), p("BI", 1, 33), STEP, A.mult, 1.0 + (1 + MID) * STEP, A.add)
+    lane_scan(p("be"), p("bx"), 32)
+    unlane(p("endl"), p("be", 15, 32, 16), 1.0)
+    cp(ix(p("NS"), p("endl")), p("zr", 0, 32))
+    fill(p("SD1", 0, 1, 1, "SD10"), 0.0)
+    fill(p("SD2", 0, 1, 1, "SD20"), 0.0)
+    relus(((0, "s"), (1, "v"), (2, "s"), (3, "v")))
+    quant_h(0)
+    send_codes(0)
+    act(p("LMr"), ix(p("RW"), p("posm")))
+    late(0)
+    act(p("tgx", 0, C), ix(p("RW"), p("posl")), F.Identity, scale=STEP, bias=1.0 + 192 * STEP)
+    targets_row()
+    ts(p("P0", 3, 4 * C, 4, "P0m"), p("LMr"), p("lane"), A.is_equal)
+    signed()
+    targets(0)
+    send_targets(0)
+    resolve(0)
+    resolve_late(0)
+    ts(p("cT"), p("m16"), p("lane"), A.add)
+    for b in range(4):
+        quant(p("ebq%d" % b), p("ebs%d" % b), p("EBW", 3 - b, 515 - b))
+    act(p("xio"), p("iota4"), F.Identity, scale=STEP, bias=1.0)
+    act(p("pir"), p("half", 0, CS), F.Identity, scale=0.0, bias=1.0 + (4 * C + 3) * STEP)
+    between(0)
+    cp(ix(p("pir"), p("rk")), p("xio"))
+    lane_scan(p("pis"), p("pir"), CS)
+    unlane(p("pi4"), p("pis", 15, CS, 16))
+
+    for t in (1, 2):
+        merge(t)
+        quant_x(t)
+        planes(t, "s", (0, 1, 2))
+        scores(t)
+        scores_late(t)
+        planes(t, "v", (3,))
+        if t == 1:
+            quant(p("vq"), p("vs"), p("VT"))
+        rise(t)
+        entries()
+        late(t)
+        runs_end()
+        gather_e(t, ((0, "s"), (2, "v"), (1, "s"), (3, "v")))
+        targets_row()
+        layer(t)
+        signed()
+        relus(((0, "s"), (1, "v"), (2, "s"), (3, "v")))
+        older_unpacked(t)
+        quant_h(t)
+        send_codes(t)
+        targets(t)
+        send_targets(t)
+        resolve(t)
+        resolve_late(t)
+        between(t)
+    act(p("OLr"), ix(p("iotaj", 0, 400, 1, ["iotaj", "iotajp"]), p("el")))
+    dma("y", [(T.ol[:, :], T.OLr[0:128:16, :])], "dol", ["OLr"], [])
+
+    merge(3)
+    H = C // 2
+    for h, bank in enumerate(("py", "py2")):
+        a, e = H * h, H * h + H
+        quant(p("xq3", a, e, 1, "xq3%d" % h), p("xs3", a, e, 1, "xs3%d" % h), p("XT3", 4 * a, 4 * e, 1, XT(3)[1]))
+        mm(p(bank, 0, H), p("vq"), p("vs"), p("xq3", a, e, 1, "xq3%d" % h), p("xs3", a, e, 1, "xs3%d" % h))
+        dma("y", [(T.oc[:, 4 * a:4 * e], T.xq3[:, a:e].bitcast(dt.uint8))], "doc%d" % h, ["xq3%d" % h], [])
+    act(p("YT", 0, H, 1, "YT0"), p("py", 0, H))
+    cp(p("YT", H, C, 1, "YT1"), p("py2", 0, H))
+    dma("s", [(T.y[:, 0:H], T.YT[:, 0:H])], "dy0", ["YT0"], [])
+    dma("y", [(T.osc[4 * k:4 * k + 4, :], T.xs3[32 * k:32 * k + 4, :]) for k in range(4)], "dos", ["xs30", "xs31"], [])
+    dma("y", [(T.y[:, H:C], T.YT[:, H:C])], "dy1", ["YT1"], [])
+    for sem in sorted(total):
+        if waited.get(sem, 0) < total[sem]:
+            g.wait_ge(T.sem[sem], total[sem])

@@ -3,13 +3,13 @@ from concourse.mybir import dt, AluOpType as A, ActivationFunctionType as F
 
 C, K, N = 384, 160, 8
 HALF = K // 2
-CV = C + 15
+H = C // 2
+CV = C + 16
 CS = C + 32
 MID = 208
 NZ = 4 * C + 4
 M1, V1, WEND = 400, 560, 1360
 LT = 10
-STEP = 2.0 ** -11
 R1 = 1.5 * 2.0 ** 23
 F32, BF, I32, U16, COD, U8 = "float32", "bfloat16", "int32", "uint16", "float8_e4m3fn_x4", "uint8"
 SCRATCH = {}
@@ -29,44 +29,44 @@ for _t in range(4):
     _b("XD%d" % _t, K, BF)
     _b("WB%d" % _t, WEND, BF)
 for _t in range(3):
-    for _n, _w, _d in [("hq", K, COD), ("hs", K, U8), ("hl", K, COD), ("hls", K, U8), ("tm", LT, U16), ("wm", 64, BF),
-                       ("lt", LT, U16), ("lw", 64, BF), ("rc", HALF, COD), ("rs", K, U8), ("rt", LT, U16), ("rw", 64, BF)]:
+    for _n, _w, _d in [("eq", K, COD), ("es", K, U8), ("ql", K, COD), ("qls", K, U8), ("hq", K, COD), ("hs", K, U8), ("wm", 64, BF),
+                       ("le", LT, U16), ("lw", 64, BF), ("rc", HALF, COD), ("rs", K, U8), ("rt", LT, U16), ("rw", 64, BF)]:
         _b("%s%d" % (_n, _t), _w, _d)
 for _n, _w, _d in [
         ("UT", 512, BF), ("VT", 512, BF), ("uq", 128, COD), ("us", 128, U8), ("ur", 128, COD), ("urs", 128, U8),
         ("ul", 128, COD), ("uls", 128, U8), ("vq", 128, COD), ("vs", 128, U8), ("wq", 512, COD), ("wsp", 512, U8),
-        ("tgT", 24, I32), ("RW", 2 * C, BF), ("tg2s", 48, BF), ("tl", 24, I32), ("lanep", 1, I32), ("lanei", 1, I32), ("half", 516, BF),
-        ("EBW", 516, BF), ("vi", 24, I32), ("ET", 4 * K, BF), ("eq", K, COD), ("es", K, U8), ("HT", 4 * K, BF), ("OLr", K, F32),
-        ("YT", C, F32)]:
+        ("rwq", 128, COD), ("rws", 128, U8), ("wl", 512, COD), ("wls", 512, U8), ("rtg", 24, U16), ("tgp", 24, U16),
+        ("tgT", 24, I32), ("lanep", 1, I32), ("lanei", 1, I32), ("half", 576, BF),
+        ("EBW", 516, BF), ("vi", 24, I32), ("ET", 4 * K, BF), ("HT", 4 * K, BF), ("OLr", K, F32), ("YT", C, F32)]:
     _b(_n, _w, _d)
 PLACE, _end = {}, {}
 for _n, _w, _d in [
-        ("lane", 1, F32), ("lane48", 1, F32), ("vini", 1, F32), ("thr", 1, F32), ("sc", 1, F32), ("scA", 1, F32), ("m16", 24, F32),
-        ("m24", 24, F32), ("x36", 36, F32), ("xf", 36, F32), ("q1", 36, F32), ("fl", 36, F32), ("q2", 36, F32), ("q3", 36, F32),
+        ("lane", 1, F32), ("vini", 1, F32), ("thr", 1, F32),
+        ("x36", 36, F32), ("xf", 36, F32), ("q1", 36, F32), ("fl", 36, F32), ("q2", 36, F32), ("q3", 36, F32),
         ("q4", 36, F32), ("q5", 36, F32), ("q6", 36, F32), ("RL", 36, U16), ("PL", 36, U16), ("KC", 576, BF), ("i16", CS, BF),
-        ("iota4", C, F32), ("xio", C, F32), ("IOTA", 400, F32), ("iotaj", 400, F32), ("mt16", 16, F32), ("D2", CS, BF), ("own", 16, BF),
-        ("hlf", 16, BF), ("pw", 16, F32), ("nr24", 576, BF), ("nr16", 32, F32), ("ones32", 32, F32), ("lu", 8, U16), ("ll", 8, U16),
-        ("nT", 24, F32), ("posl", 24, U16), ("posm", 24, U16), ("zr", 416, BF), ("ngc", 400, BF),
-        ("cT", 24, F32), ("OH", 576, BF), ("C1", 576, BF), ("Hh", 32, F32), ("HT1", 32, F32), ("PI", 32, F32), ("G1", 64, F32),
+        ("xio", CV, F32), ("I32", CV, F32), ("iotaj", CV, F32), ("Lr", 16, F32), ("D2", CS, BF), ("own", 16, BF),
+        ("pw", 16, F32), ("nr24", 576, BF), ("nr16", 32, F32), ("ones32", 32, F32), ("lu", 8, U16), ("ll", 8, U16),
+        ("zr", CV, BF), ("DR", CV, BF), ("tgu", 24, U16), ("OH", 576, BF), ("C1", 576, BF), ("Hh", 32, F32), ("HT1", 32, F32), ("PI", 32, F32), ("G1", 64, F32),
         ("GT", 64, F32), ("BI", 33, F32), ("G2", 24, F32), ("C2", 576, BF), ("C2m", 576, BF), ("NOm", 576, BF),
-        ("SEL", 576, BF), ("rk", 24, U16), ("pir", CS, F32), ("pis", CS, F32), ("pi4", 26, U16), ("bx", 32, F32), ("be", 32, F32),
-        ("endl", 2, U16), ("tgx", 400, F32), ("LMr", C, BF), ("NS", CS, BF), ("ZS0", CS, BF),
-        ("P0", 1600, BF), ("P1", 1600, BF), ("Z", 1600, BF), ("RQ", 400, BF), ("PS", 400, F32),
-        ("ac1", 1, F32), ("al", 1, U16), ("TA", 16, F32), ("FF", 17, F32), ("FD", 16, F32), ("el", 10, U16),
-        ("ZS", CS, BF), ("SD1", CS + 1, BF), ("SD2", CS + 1, BF), ("LAST", C, F32), ("junk1", 400, BF),
-        ("TT", K, F32), ("TS", K, F32), ("FX", C, F32), ("FS", C, F32), ("fl24", 24, F32), ("fvV", 24, F32),
-        ("RR", 24, F32), ("h1", 24, F32), ("d1", 24, F32), ("p1", 24, F32), ("h2", 24, F32), ("e0", 24, F32),
-        ("e1", 24, F32), ("p2", 24, F32), ("h3", 24, F32), ("qf", 24, F32), ("fin", 24, U16)]:
+        ("SEL", 576, BF), ("rk", 24, U16), ("pir", CS, F32), ("pis", CS, F32), ("pia", 14, U16), ("pib", 12, U16), ("bx", 32, F32), ("be", 32, F32),
+        ("endl", 2, U16), ("tgx", CV, F32), ("NS", CS, BF),
+        ("P0", 1600, BF), ("P1", 1600, BF), ("Z", 1600, BF), ("RQ", CV, BF), ("ST", CV, F32),
+        ("ac1", 1, F32), ("al", 1, U16), ("TA", 16, F32), ("FF", 16, F32), ("el0", LT, U16), ("el1", LT, U16), ("el2", LT, U16),
+        ("lt0", LT, U16), ("lt1", LT, U16), ("lt2", LT, U16),
+        ("ZS", CS, BF), ("SD1", CS + 1, BF), ("SD2", CS + 1, BF), ("LAST", C, F32), ("junk1", CV, BF),
+        ("TT", K, F32), ("TS", K, F32), ("FX", C, BF), ("FS", C, BF), ("DA", C, BF), ("thr2", 1, F32), ("fl24", 24, F32), ("fvV", 24, F32),
+        ("F0", 72, F32), ("F1", 72, F32), ("FQ", 72, F32), ("h2", 24, F32), ("e0", 24, F32),
+        ("e1", 24, F32), ("fin", 24, U16)]:
     PLACE[_n] = ("pack_" + _d, _end.get(_d, 0), _w)
     _end[_d] = _end.get(_d, 0) + (_w + 31) // 32 * 32
-SCRATCH["tg2"] = ("dram", [128, 48], BF)
 for _d in _end:
     _b("pack_" + _d, _end[_d], _d)
-PSUM = ["pw0", "pw1", "pw2", "pw3", "psr", "psl", "py", "py2"]
+PSUM = ["pw0", "pw1", "pw2", "pw3", "psa", "psb", "psl"]
 for _n in PSUM:
     _b(_n, 512, F32, "psum")
 
-SEMAPHORES = (["cv", "cs", "ct", "cg", "dx", "du", "dtg", "dtr", "drw", "dwc", "dws", "dv", "dol", "doc0", "doc1", "dos", "dy0", "dy1", "ls", "ro"]
+SEMAPHORES = (["cv", "cs", "ct", "cg", "dxa", "dxb", "du", "dtg", "dwc", "dws", "dv", "dol", "doc0", "doc1", "dos", "dy0", "dy1", "ls", "ro",
+               "dz", "rg", "rq", "rp", "lg", "lq"]
               + ["%s%d" % (_s, _t) for _s in ("la", "lb", "lm", "ha", "rl", "rb", "rm", "rh") for _t in range(3)])
 
 
@@ -91,19 +91,26 @@ def _relay_program(g, core, role, src, dst, T, topo):
         g.remote_dma(out, in_, T.sem[sem], T.sem.ro, pid, rid, mask)
         sent[0] += n_out
 
+    if role == 3:
+        g.wait_ge(T.sem.rg, n_all)
+        fwd(T.tgp[:, 0:24], T.rtg[:, 0:24], "lg")
+    g.wait_ge(T.sem.rp, n_all // 4)
+    fwd(T.wls[:, 128 * role:128 * role + 128], T.rws[:, 0:128], "lq")
+    g.wait_ge(T.sem.rq, n_all // 4)
+    fwd(T.wl[:, 128 * role:128 * role + 128].bitcast(dt.uint8), T.rwq[:, 0:128].bitcast(dt.uint8), "lq")
     for t in range(3):
         if role == 3:
             g.wait_ge(T.sem["rb%d" % t], n_all)
-            fwd(T["lt%d" % t][:, 0:LT], T["rt%d" % t][:, 0:LT], "lb%d" % t)
+            fwd(T["le%d" % t][:, 0:LT], T["rt%d" % t][:, 0:LT], "lb%d" % t)
             for at, a, b in ((0, "rl", "la"), (32, "rm", "lm"))[:2 if t < 2 else 1]:
                 g.wait_ge(T.sem["%s%d" % (a, t)], n_all)
-                fwd(T["lw%d" % t][:, at:at + 32], T["rw%d" % t][:, at:at + 32], "%s%d" % (b, t))
+                fwd(T["lw%d" % t][:, at:at + 24], T["rw%d" % t][:, at:at + 24], "%s%d" % (b, t))
         elif role == 2:
             g.wait_ge(T.sem["rh%d" % t], n_all)
-            fwd(T["hls%d" % t][:, 0:K], T["rs%d" % t][:, 0:K], "ha%d" % t)
+            fwd(T["qls%d" % t][:, 0:K], T["rs%d" % t][:, 0:K], "ha%d" % t)
         else:
             g.wait_ge(T.sem["rh%d" % t], n_all // 2)
-            fwd(T["hl%d" % t][:, HALF * role:HALF * role + HALF].bitcast(dt.uint8), T["rc%d" % t][:, 0:HALF].bitcast(dt.uint8), "ha%d" % t)
+            fwd(T["ql%d" % t][:, HALF * role:HALF * role + HALF].bitcast(dt.uint8), T["rc%d" % t][:, 0:HALF].bitcast(dt.uint8), "ha%d" % t)
     g.wait_ge(T.sem.ro, sent[0])
 
 
@@ -196,11 +203,23 @@ def rank_program(g, core, T, topo):
     def act(out, in_, func=F.Copy, **kw):
         op("s", lambda: s.activation(out[0], in_[0], func, **kw), [out], [in_])
 
+    def sfill(out, n, c):
+        if c:
+            act(out, p("half", 0, n), F.Identity, scale=0.0, bias=c)
+        else:
+            act(out, p("half", 0, n), scale=0.0)
+
     def signs(junk, in_, bias, accum):
         op("s", lambda: s.activation(junk[0], in_[0], F.Sign, bias=bias[0], accum_out=accum[0], scale=-1.0), [junk, accum], [in_, bias])
 
     def copy(q, out, in_):
         (cp if q == "v" else act)(out, in_)
+
+    def scaled(q, out, in_, c):
+        if q == "s":
+            act(out, in_, scale=c)
+        else:
+            ts(out, in_, c, A.mult)
 
     def quant(c, sc, in_):
         op("v", lambda: v.quantize_mx(c[0], sc[0], in_[0]), [c, sc], [in_])
@@ -215,159 +234,88 @@ def rank_program(g, core, T, topo):
         scan(out, p("D2", 0, n), row, 0.0, A.mult, A.max)
 
     def unlane(out, rows, off=0.0):
-        ts(out, rows, p("scA"), A.mult, -2048.0 - off, A.add)
+        ts(out, rows, p("pw", 15, 16), A.mult, -2048.0 - off, A.add)
 
-    def XT(t, b=None):
-        return p("XT%d" % t, 0, 4 * C, 1, ["XT%d_%d" % (t, i) for i in range(4)]) if b is None else p("XT%d" % t, b, 4 * C, 4, "XT%d_%d" % (t, b))
+    def XT(t, b=None, h=None):
+        if b is not None:
+            return p("XT%d" % t, b, 4 * C, 4, ["XT%d_%d%d" % (t, b, i) for i in range(2)])
+        return p("XT%d" % t, 4 * H * h, 4 * H * h + 4 * H, 1, ["XT%d_%d%d" % (t, i, h) for i in range(4)])
+
+    def xq(t, h=None):
+        a, e, hs = (0, C, (0, 1)) if h is None else (H * h, H * h + H, (h,))
+        return [p("%s%d" % (n, t), a, e, 1, ["%s%d_%d" % (n, t, i) for i in hs]) for n in ("xq", "xs")]
 
     def WB(b, a, e, parts):
         return p("WB%d" % b, a, e, 1, ["W%s_%d" % (k, b) for k in parts])
 
-    dma("s", [(T.XT0[:, 0:4 * C], T.x[:, :])], "dx", [], XT(0)[1])
-    dma("y", [(T.tgT[:, :], T.tg[:, :])], "dtg", [], ["tgT"])
-    dma("y", [(T.UT[:, :], T.u[:, :])], "du", [], ["UT"])
-    dma("y", [(T.wq[:, :].bitcast(dt.uint8), T.wc[:, :])], "dwc", [], ["wq"])
-    dma("y", [(T.wsp[:, :], T.ws[:, :])], "dws", [], ["wsp"])
-    dma("y", [(T.VT[:, :], T.v[:, :])], "dv", [], ["VT"])
+    BANK = ("psa", "psb")
 
-    fill(p("half"), 0.5)
-    iota(p("lanep"), [[1, 1]], 0, 1)
-    iota(p("x36"), [[16, 36]])
-    iota(p("m16"), [[16, 24]])
-    iota(p("KC"), [[1, 24], [0, 24]])
-    iota(p("m24"), [[1, 24]])
-    iota(p("i16"), [[0, 26], [1, 16]])
-    iota(p("mt16"), [[16, 16]], -64)
-    iota(p("IOTA"), [[1, 400]])
-    for b in range(4):
-        iota(WB(b, C, M1, "0"), [[0, 16]])
-    op("g", lambda: g.affine_select(T.EBW[:, :], T.half[:, :], [[1, 516]], A.is_equal, 0.0, -3, -4), [p("EBW")], [p("half")])
-    iota(p("NS"), [[0, CS]], 1)
-    iota(p("ZS0"), [[0, CS]])
-    iota(p("iota4"), [[4, C]], 3)
-    iota(p("iotaj", 0, C), [[1, C]])
-    iota(p("iotaj", C, 400, 1, "iotajp"), [[0, 16]], -1)
-
-    ts(p("lanei"), p("lanep"), 15, A.bitwise_and)
-    fill(p("Hh"), 0.0)
-    cp(p("lane"), p("lanei"))
-    fill(p("ones32"), 1.0)
-    ts(p("xf"), p("x36"), p("lane"), A.add)
-    fill(p("hlf"), 0.5)
-    fill(p("nr24"), 1.0)
-    fill(p("BI", 0, 1, 1, "BI0"), -1.0 - MID)
-    fill(p("P0", 4 * C + 2, 4 * C + 4, 1, "P0z"), 0.0)
-    ts(p("P0", 4 * C + 1, 4 * CV, 4, "P0v"), p("hlf", 0, 15), 2.0, A.mult)
-    ts(p("q1"), p("xf"), 1.0 / 24, A.mult, -11.5 / 24, A.add)
-    ts(p("q3"), p("xf"), -24.0, A.mult, 552.0, A.add)
-    ts(p("fl"), p("q1"), R1, A.add, R1, A.subtract)
-    ts(p("q2"), p("fl"), -24.0, A.mult)
-    ts(p("q4"), p("fl"), 577.0, A.mult)
-    tt(p("q5"), p("q2"), p("xf"), A.add)
-    tt(p("q6"), p("q4"), p("q3"), A.add)
-    cp(p("RL"), p("q5"))
-    cp(p("PL"), p("q6"))
-    ts(p("tl"), p("tgT"), 15, A.bitwise_and)
-    ts(p("tg2s", 0, 24, 1, "tg2a"), p("tgT"), -192.0, A.add)
-    cp(p("tg2s", 24, 48, 1, "tg2b"), p("tl"))
-    dma("y", [(T.tg2[:, :], T.tg2s[:, :])], "dtr", ["tg2a", "tg2b"], ["tg2"])
-    dma("y", [(T.RW[i:128:16, :], T.tg2[:, :]) for i in range(16)], "drw", ["tg2"], ["RW"])
-    ts(p("vi"), p("tgT"), 4, A.arith_shift_right)
-    tt(p("OH"), ix(p("vi"), p("RL")), p("KC"), A.is_equal)
-    ts(p("nr24", 0, 576, 24), p("nr24", 0, 576, 24), 0.0, A.mult)
-    scan(p("C1"), p("nr24"), p("OH"), 0.0, A.mult, A.add)
-    cp(p("Hh", 0, 24), p("C1", 23, 576, 24))
-    turn(p("HT1"), p("Hh"))
-    cp(p("lu"), p("m16", 0, 8))
-    quant(p("uq"), p("us"), p("UT"))
-    cp(cast(p("ur"), dt.uint32), ix(cast(p("uq"), dt.uint32), p("lu")))
-    for i in range(3):
-        act(p("P1", 516 * i, min(516 * i + 516, NZ), 1, "P1"), p("half", 0, min(516, NZ - 516 * i)), scale=0.0)
-    act(p("P0", 0, NZ, 4, "P0"), p("half", 0, C + 1), scale=0.0)
-    act(p("ngc"), p("half", 0, 400), F.Identity, scale=0.0, bias=-2064.0 - 80.0)
-    act(p("zr"), p("half", 0, 416), scale=0.0)
-    act(p("NOm"), ix(p("OH"), p("PL")), scale=-1000.0)
-    act(p("urs"), ix(p("us"), p("lu")))
-
-    def quant_x(t):
-        quant(p("xq%d" % t), p("xs%d" % t), XT(t))
+    def quant_x(t, h):
+        quant(*xq(t, h), XT(t, None, h))
 
     def planes(t, q, bs):
         for b in bs:
-            copy(q, WB(b, 0, C, "X"), XT(t, b))
+            o, i = WB(b, 0, C, "X"), XT(t, b)
+            if q == "g":
+                op("g", lambda: g.affine_select(o[0], i[0], [[0, C]], A.is_equal, 0.0, 0, 0), [o], [i])
+            else:
+                copy(q, o, i)
 
-    def scores(t):
-        mm(p("psr", 0, C), p("ur"), p("urs"), p("xq%d" % t), p("xs%d" % t))
+    def scores(t, h):
+        mm(p(BANK[h], 0, H), p("ur"), p("urs"), *xq(t, h))
 
     def scores_late(t):
-        mm(p("psl", 0, C), p("ul"), p("uls"), p("xq%d" % t), p("xs%d" % t))
+        mm(p("psl", 0, C), p("ul"), p("uls"), *xq(t))
 
-    def rise(t):
-        tt(p("P0", 1, 4 * C, 4, "P0r"), p("psr", 0, C), p("LAST"), A.is_gt)
+    def rise(t, h):
+        o = p("P0", 4 * H * h + 1, 4 * H * h + 4 * H, 4, "P0r%d" % h)
+        if t == 0:
+            ts(o, p(BANK[h], 0, H), 0.0, A.is_gt)
+        else:
+            tt(o, p(BANK[h], 0, H), p("LAST", H * h, H * h + H, 1, "LAST%d" % h), A.is_gt)
+
+    FLAGS = ["P0", "P0r0", "P0r1", "P0v"]
 
     def entries():
-        flags = p("P0", 1, 4 * CV, 4, ["P0", "P0r", "P0v"])
+        flags = p("P0", 1, 4 * CV, 4, FLAGS)
         scan(p("P1", 0, 4 * CV, 4, "P1y"), flags, (p("zr", 0, CV)[0], ["zr", "P1"]), -161.0, A.add, A.min)
-        signs(p("junk1", 0, CV), p("P1", 0, 4 * CV, 4, "P1y"), p("thr"), p("ac1"))
-        scan(p("RQ", 0, CV), flags, p("zr", 0, CV), p("vini"), A.add, A.add)
-        scan(p("PS", 1, 1 + CV), p("RQ", 0, CV), p("ngc", 0, CV), 0.0, A.add, A.add)
+        signs(p("junk1", 0, CV - 1), p("P1", 0, 4 * CV - 4, 4, "P1y"), p("thr"), p("ac1"))
+        scan(p("RQ"), flags, p("zr", 0, CV), p("vini"), A.add, A.add)
+        scan(p("ST"), p("DR"), p("RQ"), 0.0, A.add, A.max)
 
-    def runs_end():
-        ts(p("al"), p("ac1"), float(CV), A.add, 0.5, A.mult)
-        tt(p("TA"), ix(p("IOTA"), p("al")), p("mt16"), A.mult)
-        tt(p("FF", 1, 17), ix(p("PS", 0, 400, 1, ["PS", "PS0"]), p("al")), p("TA"), A.subtract)
-        tt(p("FD"), p("FF", 0, 16, 1, ["FF", "FF0"]), p("FF", 1, 17), A.subtract)
-        ts(p("el"), p("FD", 0, 10), 1.0 / 16, A.mult)
+    def runs_end(t):
+        ts(p("al"), p("ac1"), float(CV - 1), A.add, 0.5, A.mult)
+        tt(p("TA"), ix(p("ST"), p("al")), p("Lr"), A.subtract)
+        tt(p("FF"), ix(p("I32"), p("al")), p("TA"), A.subtract)
+        ts(p("el%d" % t), p("FF", 0, LT), 32.0, A.mult, float(CV - 1), A.min)
+        send_list(p("el%d" % t), T["rt%d" % t][:, 0:LT], "rb%d" % t)
 
-    def late(t):
+    def late():
         o = p("P0", 2, 4 * C, 4, "P0l")
         op("s", lambda: s.activation(o[0], p("psl", 0, C)[0], F.Sign, bias=-2.0 ** -118), [o], [p("psl")])
 
     def signed():
-        scan(p("Z", 0, NZ), p("P0", 0, NZ, 1, ["P0", "P0r", "P0v", "P0l", "P0m", "P0z"]), p("P1", 0, NZ, 1, ["P1", "P1y"]), 0.0, A.mult, A.add)
+        scan(p("Z", 0, NZ), p("P0", 0, NZ, 1, FLAGS + ["P0l", "P0m", "P0z"]), p("P1", 0, NZ, 1, ["P1", "P1y"]), 0.0, A.mult, A.add)
 
     def resolve(t):
-        if t == 0:
-            cp(ix(p("ZS0"), p("rk")), p("Z", 3, 4 * C, 4))
-        else:
-            cp(p("ZS"), ix(p("Z", 0, NZ), p("pi4")))
-        scan(p("SD1", 1, CS + 1), p("NS"), p("ZS" if t else "ZS0"), 0.0, A.mult, A.max)
-        act(p("wm%d" % t, 0, 32, 1, "wm%da" % t), ix(p("SD1", 0, CS, 1, ["SD1", "SD10"]), p("endl")))
-        send_winners(t, "a", 0, "rl")
-
-    def resolve_late(t):
-        act(p("FX"), p("Z", 1, 4 * C, 4), F.Identity, scale=-(2.0 ** -8), bias=1.0)
+        act(p("ZS", 224, CS, 1, "ZSb"), ix(p("Z", 0, NZ), p("pib")))
+        cp(p("ZS", 0, 224, 1, "ZSa"), ix(p("Z", 0, NZ), p("pia")))
+        zs = p("ZS", key=["ZSa", "ZSb"])
+        scan(p("SD1", 1, CS + 1), p("NS"), zs, 0.0, A.mult, A.max)
+        cp(p("wm%d" % t, 0, 32, 1, "wm%da" % t), ix(p("SD1", 0, CS, 1, ["SD1", "SD10"]), p("endl")))
+        send_list(p("wm%d" % t, 0, 24, 1, "wm%da" % t), T["rw%d" % t][:, 0:24], "rl%d" % t)
         if t < 2:
-            scan(p("SD2", 1, CS + 1), p("NS"), p("ZS" if t else "ZS0"), 0.0, A.mult, A.min)
-            act(p("wm%d" % t, 32, 64, 1, "wm%db" % t), ix(p("SD2", 0, CS, 1, ["SD2", "SD20"]), p("endl")), scale=-1.0)
-            send_winners(t, "b", 32, "rm")
+            scan(p("SD2", 1, CS + 1), p("NS"), zs, 0.0, A.mult, A.min)
+            ts(p("wm%d" % t, 32, 64, 1, "wm%db" % t), ix(p("SD2", 0, CS, 1, ["SD2", "SD20"]), p("endl")), -1.0, A.mult)
+            send_list(p("wm%d" % t, 32, 56, 1, "wm%db" % t), T["rw%d" % t][:, 32:56], "rm%d" % t)
 
     def gather_e(t, pairs):
         for b, q in pairs:
-            copy(q, p("ET", b, None, 4, "ET%d" % b), ix(WB(b, 0, M1, "X0"), p("el")))
+            copy(q, p("ET", b, None, 4, "ET%d" % b), ix(WB(b, 0, M1, "X0"), p("el%d" % t)))
 
-    def layer(t):
-        quant(p("eq"), p("es"), p("ET", 0, None, 1, ["ET%d" % b for b in range(4)]))
-        for b in range(4):
-            mm(p("pw%d" % b, 0, K), p("wq", 128 * b, 128 * b + 128), p("wsp", 128 * b, 128 * b + 128), p("eq"), p("es"))
-
-    def targets_row():
-        act(p("TT"), ix(p("tgx", 0, 400, 1, ["tgx", "tgxp"]), p("el")))
-
-    def targets(t):
-        lane_scan(p("TS"), p("TT"), K)
-        unlane(p("tm%d" % t), p("TS", 15, K, 16))
-
-    def relus(pairs):
-        for b, q in pairs:
-            o, i = p("HT", b, None, 4, "HT%d" % b), p("pw%d" % b, 0, K)
-            if q == "s":
-                act(o, i, F.Relu, scale=0.03125)
-            else:
-                ts(o, i, 0.0, A.max, 0.03125, A.mult)
-
-    def quant_h(t):
-        quant(p("hq%d" % t), p("hs%d" % t), p("HT", 0, None, 1, ["HT%d" % b for b in range(4)]))
+    def quant_e(t):
+        quant(p("eq%d" % t), p("es%d" % t), p("ET", 0, None, 1, ["ET%d" % b for b in range(4)]))
+        send_codes(t)
 
     rel = _relays(rank, T, topo)
 
@@ -376,63 +324,78 @@ def rank_program(g, core, T, topo):
         g.remote_dma(out, in_, T.sem[sem], T.sem.ls, pid, rid, topo.mask(core, rel[i]))
         total["ls"] = total.get("ls", 0) + len(topo.engines(core, rel[i]))
 
-    def send_codes(t):
-        deps("g", ["hq%d" % t, "hs%d" % t], [])
+    def share(srcs, dst, sem):
         es = topo.engines(core, rel[0])
-        h, tr = len(es) // 2, []
-        for i in range(2):
+        h, tr = len(es) // len(srcs), []
+        for i, src in enumerate(srcs):
             rid, pid = topo.addr(rel[i], core)
-            tr.append(RemoteDMATransfer(dst_ids=[DstId(rid=rid, pnc=pid)], dma_engine_mask=_bits(es[h * i:h * i + h]), remote_sem=T.sem["rh%d" % t],
-                                        src=T["hq%d" % t][:, HALF * i:HALF * i + HALF].bitcast(dt.uint8), dst=T["rc%d" % t][:, 0:HALF].bitcast(dt.uint8)))
+            tr.append(RemoteDMATransfer(dst_ids=[DstId(rid=rid, pnc=pid)], dma_engine_mask=_bits(es[h * i:h * i + h]), remote_sem=T.sem[sem], src=src, dst=dst))
         g.remote_dma_fused(tr, local_sem=T.sem.ls)
-        total["ls"] = total.get("ls", 0) + 2 * h
-        send(2, T["rs%d" % t][:, 0:K], T["hs%d" % t][:, 0:K], "rh%d" % t)
+        total["ls"] = total.get("ls", 0) + len(es)
 
-    def send_targets(t):
-        deps("g", ["tm%d" % t], [])
-        send(3, T["rt%d" % t][:, 0:LT], T["tm%d" % t][:, 0:LT], "rb%d" % t)
+    def send_codes(t):
+        deps("g", ["eq%d" % t, "es%d" % t], [])
+        share([T["eq%d" % t][:, HALF * i:HALF * i + HALF].bitcast(dt.uint8) for i in range(2)], T["rc%d" % t][:, 0:HALF].bitcast(dt.uint8), "rh%d" % t)
+        send(2, T["rs%d" % t][:, 0:K], T["es%d" % t][:, 0:K], "rh%d" % t)
 
-    def send_winners(t, k, at, sem):
-        deps("g", ["wm%d%s" % (t, k)], [])
-        send(3, T["rw%d" % t][:, at:at + 32], T["wm%d" % t][:, at:at + 32], "%s%d" % (sem, t))
+    def send_list(src, dst, sem):
+        deps("g", src[1], [])
+        send(3, dst, src[0], sem)
 
-    def between(t):
-        n = t + 1
-        if t < 2:
-            act(p("LAST"), p("psr", 0, C))
-        if n >= 2:
-            for b in range(4):
-                tt(WB(b, V1 + 320 * (t - 1), V1 + 320 * (t - 1) + K, ["A%d" % (t - 1)]), p("pw%d" % b, 0, K), p("XD%d" % b), A.add)
-        lane_scan(p("FS"), p("FX"), C)
-        ts(p("fl24"), p("FS", 15, C, 16), p("sc"), A.mult, 1.0, A.is_gt)
-        ts(p("fvV"), p("fl24"), 160.0, A.mult, float(V1 + 320 * t), A.add)
-        if n >= 2:
-            older = p("lw%d" % (t - 1), 32, 56, 1, "lx%d" % (t - 1))
-            ts(p("h2"), older, 0.0, A.is_gt)
-            ts(p("e0"), older, -1.0, A.mult, -320.0, A.add)
-            tt(p("e1"), p("e0"), p("fvV"), A.add)
-            tt(p("p2"), p("e1"), p("h2"), A.mult)
-            tt(p("RR"), p("p2"), p("cT"), A.max)
-            ts(p("h3"), p("h2"), -8192.0, A.mult)
-            tt(p("fvV"), p("fvV"), p("h3"), A.add)
+    def unpack(t):
+        for b in range(4):
+            mm(p("pw%d" % b, 0, K), p("ebq%d" % b), p("ebs%d" % b), p("hq%d" % t), p("hs%d" % t))
 
-    def older_unpacked(t):
+    def fired(t):
+        act(p("FX"), p("Z", 1, 4 * C, 4), F.Sign, scale=-1.0)
+        scan(p("FS"), p("DA"), p("FX"), 0.0, A.add, A.max)
+        ts(p("fl24"), p("FS", 15, C, 16), p("thr2"), A.is_gt, 160.0, A.mult)
+        ts(p("fvV"), p("fl24"), float(V1 + 320 * t), A.add)
+        if t >= 1:
+            was = p("lw%d" % (t - 1), 32, 56, 1, "lx%d" % (t - 1))
+            ts(p("e0"), p("fl24"), float(V1 + 320 * (t - 1)), A.add)
+            ts(p("h2"), was, 0.0, A.is_gt)
+            tt(p("e1"), p("e0"), was, A.subtract)
+            ts(p("F0", 2, 72, 3, "F0o"), was, 0.0, A.is_le)
+            tt(p("F1", 2, 72, 3, "F1o"), p("e1"), p("h2"), A.mult)
+
+    def last():
+        for h in range(2):
+            act(p("LAST", H * h, H * h + H, 1, "LAST%d" % h), p(BANK[h], 0, H))
+
+    def older(t):
+        unpack(t - 1)
         for b in range(4):
             act(p("XD%d" % b), ix(WB(b, 0, M1, ["X", "0"]), p("lt%d" % (t - 1))), scale=0.5)
         for b in range(4):
-            mm(p("pw%d" % b, 0, K), p("ebq%d" % b), p("ebs%d" % b), p("hl%d" % (t - 1)), p("hls%d" % (t - 1)))
+            tt(WB(b, V1 + 320 * (t - 1), V1 + 320 * (t - 1) + K, ["A%d" % (t - 1)]), p("pw%d" % b, 0, K), p("XD%d" % b), A.add)
+
+    def targets(t):
+        act(p("TT"), ix(p("tgx", key=["tgx", "tgxp"]), p("le%d" % t)))
+        lane_scan(p("TS"), p("TT"), K)
+        unlane(p("lt%d" % t), p("TS", 15, K, 16))
+
+    def halves(t):
+        for b, q in ((0, "v"), (1, "s"), (2, "v"), (3, "s")):
+            scaled(q, p("XG%d" % b), ix(WB(b, 0, M1, ["X", "0"]), p("lt%d" % t)), 0.5)
 
     def merge(n):
         t = n - 1
-        lw, lt, m, a = "lw%d" % t, "lt%d" % t, M1 + 320 * t, V1 + 320 * t
-        for b, q in ((0, "s"), (3, "v"), (1, "s"), (2, "s")):
-            o, i = p("XG%d" % b), ix(WB(b, 0, M1, ["X", "0"]), p(lt))
-            if q == "s":
-                act(o, i, scale=0.5)
-            else:
-                ts(o, i, 0.5, A.mult)
+        lw, m, a = p("lw%d" % t, 0, 24), M1 + 320 * t, V1 + 320 * t
         for b in range(4):
-            mm(p("pw%d" % b, 0, K), p("ebq%d" % b), p("ebs%d" % b), p("hl%d" % t), p("hls%d" % t))
+            mm(p("pw%d" % b, 0, K), p("wl", 128 * b, 128 * b + 128), p("wls", 128 * b, 128 * b + 128), p("ql%d" % t), p("qls%d" % t))
+        for b, q in ((0, "v"), (1, "s"), (2, "v"), (3, "s")):
+            o, i = p("HT", b, None, 4, "HT%d" % b), p("pw%d" % b, 0, K)
+            if q == "s":
+                act(o, i, F.Relu, scale=0.03125)
+            else:
+                ts(o, i, 0.0, A.max, 0.03125, A.mult)
+        quant(p("hq%d" % t), p("hs%d" % t), p("HT", 0, None, 1, ["HT%d" % b for b in range(4)]))
+        unpack(t)
+        ts(p("F0", 1, 72, 3, "F0h"), lw, 0.0, A.is_gt)
+        tt(p("F1", 0, 72, 3, "F1d"), p("fvV"), lw, A.subtract)
+        scan(p("FQ"), p("F0", key=["F0", "F0h", "F0o"]), p("F1", key=["F1d", "F1c", "F1o"]), 0.0, A.mult, A.max)
+        cp(p("fin"), p("FQ", 2, 72, 3))
 
         def mean(b):
             tt(WB(b, a, a + K, ["A%d" % t]), p("pw%d" % b, 0, K), p("XG%d" % b), A.add)
@@ -440,135 +403,185 @@ def rank_program(g, core, T, topo):
         def move(b):
             act(WB(b, m, m + K, ["M%d" % t]), p("pw%d" % b, 0, K), scale=2.0)
 
-        def final():
-            ts(p("h1"), p(lw, 0, 24), 0.0, A.is_gt)
-            tt(p("d1"), p("fvV"), p(lw, 0, 24), A.subtract)
-            tt(p("p1"), p("d1"), p("h1"), A.mult)
-            tt(p("qf"), p("p1"), p("cT" if n == 1 else "RR"), A.max)
-            cp(p("fin"), p("qf"))
-
-        mean(0), move(1), mean(2), move(3), mean(1), move(0)
-        final()
-        mean(3), move(2)
-        for b, q in ((0, "v"), (1, "s"), (2, "v"), (3, "s")):
+        mean(0), move(1), mean(2), move(3), mean(1), move(0), mean(3), move(2)
+        for b, q in ((0, "s"), (1, "v"), (2, "s"), (3, "v")):
             copy(q, XT(n, b), ix(WB(b, 0, a + K, ["X", "0"] + ["%s%d" % (k, i) for i in range(n) for k in "MA"]), p("fin")))
 
+    arrivals = [("lg", 8, ["tgp"]), ("lq", 64, ["wl", "wls"])]
     for t in range(3):
-        for sem, n, keys in (("lb", 8, ["lt%d" % t]), ("la", 8, ["lw%d" % t]), ("lm", 8, ["lx%d" % t]), ("ha", 24, ["hl%d" % t, "hls%d" % t])):
-            if sem == "lm" and t == 2:
-                continue
-            total["%s%d" % (sem, t)] = n
-            note("%s%d" % (sem, t), None, [], keys)
+        arrivals += [("lb%d" % t, 8, ["le%d" % t]), ("la%d" % t, 8, ["lw%d" % t]), ("ha%d" % t, 24, ["ql%d" % t, "qls%d" % t])]
+        arrivals += [("lm%d" % t, 8, ["lx%d" % t])] if t < 2 else []
+    for sem, n, keys in arrivals:
+        total[sem] = n
+        note(sem, None, [], keys)
 
-    quant_x(0)
-    scores(0)
-    ts(p("nr16"), p("i16", 0, 32), 0.0, A.is_gt)
+    dma("s", [(T.tgT[:, :], T.tg[:, :])], "dtg", [], ["tgT"])
+    dma("y", [(T.UT[:, :], T.u[:, :])], "du", [], ["UT"])
+    dma("s", [(T.XT0[:, 0:4 * H], T.x[:, 0:4 * H])], "dxa", [], XT(0, None, 0)[1])
+    dma("y", [(T.XT0[:, 4 * H:4 * C], T.x[:, 4 * H:4 * C])], "dxb", [], XT(0, None, 1)[1])
+
+    fill(p("half"), 0.5)
+    fill(p("zr"), 0.0)
+    iota(p("lanep"), [[1, 1]], 0, 1)
+    iota(p("x36"), [[16, 36]])
+    iota(p("KC"), [[1, 24], [0, 24]])
+    iota(p("i16"), [[0, 26], [1, 16]])
+    dma("y", [(T.pack_bfloat16[:, PLACE["P1"][1] + 400 * i:PLACE["P1"][1] + 400 * i + 400], p("zr", 0, 400)[0]) for i in range(4)], "dz", ["zr"], ["P1"])
+    dma("y", [(T.wsp[:, :], T.ws[:, :])], "dws", [], ["wsp"])
+    dma("y", [(T.wq[:, :].bitcast(dt.uint8), T.wc[:, :])], "dwc", [], ["wq"])
+    sfill(p("nr24"), 576, 1.0)
+    sfill(p("nr24", 0, 576, 24), 24, 0.0)
+    sfill(p("Hh"), 32, 0.0)
+    sfill(p("nr16"), 32, 1.0)
+    sfill(p("ones32"), 32, 1.0)
+    sfill(p("nr16", 0, 32, 16), 2, 0.0)
+    sfill(p("BI", 0, 1, 1, "BI0"), 1, -1.0 - MID)
+    sfill(p("P0", 0, NZ, 4, "P0"), C + 1, 0.0)
+    sfill(p("P0", 4 * C + 2, 4 * C + 4, 1, "P0z"), 2, 0.0)
+    sfill(p("P0", 4 * C + 1, 4 * CV, 4, "P0v"), 16, 1.0)
+    sfill(p("DR"), CV, 1.0 / 32)
+    for b in range(4):
+        sfill(WB(b, C, M1, "0"), 16, 0.0)
+    sfill(p("pir"), CS, 2048.0 + 4 * C + 3)
+    sfill(p("NS"), CS, 1.0)
+
+    ts(p("lanei"), p("lanep"), 15, A.bitwise_and)
+    cp(p("lu"), p("x36", 0, 8))
+    cp(p("lane"), p("lanei"))
+    ts(p("ll"), p("x36", 0, 8), 1.0, A.add)
+    ts(p("xf"), p("x36"), p("lane"), A.add)
+    ts(p("Lr"), p("x36", 0, 16), 2080.0, A.add)
+    ts(p("q1"), p("xf"), 1.0 / 24, A.mult, -11.5 / 24, A.add)
+    ts(p("q3"), p("xf"), -24.0, A.mult, 552.0, A.add)
+    ts(p("fl"), p("q1"), R1, A.add, R1, A.subtract)
+    ts(p("vini"), p("lane"), -1.0, A.mult, 2064.0 + 7.5, A.add)
+    ts(p("q2"), p("fl"), -24.0, A.mult)
+    ts(p("q4"), p("fl"), 577.0, A.mult)
+    tt(p("q5"), p("q2"), p("xf"), A.add)
+    tt(p("q6"), p("q4"), p("q3"), A.add)
+    cp(p("RL"), p("q5"))
+    cp(p("PL"), p("q6"))
+    ts(p("thr"), p("lane"), 16.0, A.mult, -145.5, A.add)
+    ts(p("thr2"), p("lane"), -2.0, A.mult, 30.5, A.add)
+
+    ts(p("vi"), p("tgT"), 4, A.arith_shift_right)
+    cp(p("tgu"), p("tgT"))
+    send_list(p("tgu"), T.rtg[:, 0:24], "rg")
+    iota(p("xio"), [[4, CV]], 2048 + 3)
+    planes(0, "g", (0, 1))
+    deps("g", ["wsp"], [])
+    share([T.wsp[:, 128 * i:128 * i + 128] for i in range(4)], T.rws[:, 0:128], "rp")
+    planes(0, "g", (2,))
+    deps("g", ["wq"], [])
+    share([T.wq[:, 128 * i:128 * i + 128].bitcast(dt.uint8) for i in range(4)], T.rwq[:, 0:128].bitcast(dt.uint8), "rq")
+    planes(0, "g", (3,))
+    tt(p("OH"), ix(p("vi"), p("RL")), p("KC"), A.is_equal)
+    act(p("NOm"), ix(p("OH"), p("PL")), scale=-1000.0)
+    scan(p("C1"), p("nr24"), p("OH"), 0.0, A.mult, A.add)
+    ts(p("D2"), p("i16"), p("lane"), A.not_equal, 2.0, A.mult)
+    cp(p("Hh", 0, 24), p("C1", 23, 576, 24))
+    quant(p("uq"), p("us"), p("UT"))
+    turn(p("HT1"), p("Hh"))
+    act(p("urs"), ix(p("us"), p("lu")))
+    ts(p("own"), p("D2", 0, 16), -0.5, A.mult, 1.0, A.add)
     scan(p("PI"), p("nr16"), p("HT1"), 0.0, A.mult, A.add)
+    scan(p("pw"), p("half", 0, 16), p("own"), 0.0, A.mult, A.max)
     tt(p("G1", 0, 32), p("PI"), p("HT1"), A.subtract)
     for a in range(2):
         ts(p("G1", 32 + 16 * a, 48 + 16 * a, 1, "G1%d" % a), p("ones32", 0, 16), p("PI", 16 * a + 15, 16 * a + 16), A.mult, 1.0, A.add)
+    cp(cast(p("ur"), dt.uint32), ix(cast(p("uq"), dt.uint32), p("lu")))
     turn(p("GT"), p("G1", key=["G1", "G10", "G11"]))
+    quant_x(0, 0)
+    scores(0, 0)
     scan(p("BI", 1, 33), p("ones32"), p("GT", 32, 64), -1.0 - MID, A.mult, A.add)
+    quant_x(0, 1)
+    scores(0, 1)
     tt(p("G2"), p("GT", 0, 24), p("BI", 0, 24, 1, ["BI", "BI0"]), A.add)
+    ts(p("bx"), p("BI", 1, 33), 2048.0 + 1 + MID, A.add)
     tt(p("OH", 0, 576, 24), p("OH", 0, 576, 24), p("G2"), A.add)
-    scan(p("C2"), p("nr24"), p("OH"), 0.0, A.mult, A.add)
-    planes(0, "s", (0, 1))
-    act(p("C2m"), ix(p("C2"), p("PL")))
-    ts(p("ll"), p("m16", 0, 8), 1.0, A.add)
-    ts(p("vini"), p("lane"), -1.0, A.mult, 2064.0 + 7.5, A.add)
-    ts(p("thr"), p("lane"), 16.0, A.mult, -145.5, A.add)
-    fill(p("PS", 0, 1, 1, "PS0"), 0.0)
-    fill(p("FF", 0, 1, 1, "FF0"), 0.0)
-    fill(p("tgx", C, 400, 1, "tgxp"), 1.0)
-    ts(p("P0", 1, 4 * C, 4, "P0r"), p("psr", 0, C), 0.0, A.is_gt)
-    entries()
-    runs_end()
-    planes(0, "s", (2, 3))
-    scan(p("SEL"), p("NOm"), p("C2m"), -2000.0, A.add, A.max)
-    cp(cast(p("ul"), dt.uint32), ix(cast(p("uq"), dt.uint32), p("ll")))
-    ts(p("lane48"), p("lane"), 48.0, A.mult)
-    ts(p("nT"), p("m24"), p("lane48"), A.add)
-    ts(p("posm"), p("nT"), 24.0, A.add)
-    cp(p("posl"), p("nT"))
-    gather_e(0, ((0, "s"), (2, "v"), (1, "s"), (3, "v")))
-    layer(0)
-    act(p("uls"), ix(p("us"), p("ll")))
-    scores_late(0)
-    ts(p("rk"), p("SEL", 23, 576, 24), float(MID), A.add)
-    ts(p("D2"), p("i16"), p("lane"), A.not_equal, 2.0, A.mult)
-    ts(p("own"), p("i16", 0, 16), p("lane"), A.is_equal)
-    scan(p("pw"), p("hlf"), p("own"), 0.0, A.mult, A.max)
-    cp(p("sc"), p("pw", 15, 16))
-    ts(p("scA"), p("sc"), 2048.0, A.mult)
-    ts(p("bx"), p("BI", 1, 33), STEP, A.mult, 1.0 + (1 + MID) * STEP, A.add)
     lane_scan(p("be"), p("bx"), 32)
+    scan(p("C2"), p("nr24"), p("OH"), 0.0, A.mult, A.add)
+    act(p("I32"), p("xio"), F.Identity, scale=1.0 / 128, bias=-2051.0 / 128)
+    act(p("C2m"), ix(p("C2"), p("PL")))
+    rise(0, 0)
+    rise(0, 1)
+    entries()
+    cp(cast(p("ul"), dt.uint32), ix(cast(p("uq"), dt.uint32), p("ll")))
+    act(p("uls"), ix(p("us"), p("ll")))
+    act(p("P0", 3, 4 * C, 4, "P0m"), ix(p("D2", 0, C), p("tgu")), F.Identity, scale=-0.5, bias=1.0)
+    runs_end(0)
+    dma("y", [(T.VT[:, :], T.v[:, :])], "dv", ["el0"], ["VT"])
+    scores_late(0)
+    scan(p("SEL"), p("NOm"), p("C2m"), -2000.0, A.add, A.max)
     unlane(p("endl"), p("be", 15, 32, 16), 1.0)
+    ts(p("rk"), p("SEL", 23, 576, 24), float(MID), A.add)
+    gather_e(0, ((0, "s"), (1, "s"), (2, "s"), (3, "s")))
+    late()
+    cp(ix(p("pir"), p("rk")), p("xio", 0, C))
+    quant_e(0)
+    op("g", lambda: g.affine_select(T.EBW[:, :], T.half[:, 0:516], [[1, 516]], A.is_equal, 0.0, -3, -4), [p("EBW")], [p("half")])
+    lane_scan(p("pis"), p("pir"), CS)
     cp(ix(p("NS"), p("endl")), p("zr", 0, 32))
-    fill(p("SD1", 0, 1, 1, "SD10"), 0.0)
-    fill(p("SD2", 0, 1, 1, "SD20"), 0.0)
-    relus(((0, "s"), (1, "v"), (2, "s"), (3, "v")))
-    quant_h(0)
-    send_codes(0)
-    act(p("LMr"), ix(p("RW"), p("posm")))
-    late(0)
-    act(p("tgx", 0, C), ix(p("RW"), p("posl")), F.Identity, scale=STEP, bias=1.0 + 192 * STEP)
-    targets_row()
-    ts(p("P0", 3, 4 * C, 4, "P0m"), p("LMr"), p("lane"), A.is_equal)
+    unlane(p("pib"), p("pis", 239, CS, 16))
+    unlane(p("pia"), p("pis", 15, 224, 16))
+    sfill(p("SD1", 0, 1, 1, "SD10"), 1, 0.0)
+    sfill(p("SD2", 0, 1, 1, "SD20"), 1, 0.0)
+    sfill(p("tgx", C, CV, 1, "tgxp"), 16, 2048.0)
+    act(p("DA"), p("D2", 0, C), F.Identity, scale=33.0, bias=-64.0)
     signed()
-    targets(0)
-    send_targets(0)
     resolve(0)
-    resolve_late(0)
-    ts(p("cT"), p("m16"), p("lane"), A.add)
+    iota(p("iotaj"), [[1, CV]])
+    act(p("tgx", 0, C), ix(p("xio"), p("tgp")), F.Identity, scale=0.25, bias=2048.0 - 2051.0 / 4)
     for b in range(4):
         quant(p("ebq%d" % b), p("ebs%d" % b), p("EBW", 3 - b, 515 - b))
-    act(p("xio"), p("iota4"), F.Identity, scale=STEP, bias=1.0)
-    act(p("pir"), p("half", 0, CS), F.Identity, scale=0.0, bias=1.0 + (4 * C + 3) * STEP)
-    between(0)
-    cp(ix(p("pir"), p("rk")), p("xio"))
-    lane_scan(p("pis"), p("pir"), CS)
-    unlane(p("pi4"), p("pis", 15, CS, 16))
+    fired(0)
+    last()
+    fill(p("F0", 0, 72, 3), 0.0)
+    fill(p("F0", 2, 72, 3, "F0o"), 1.0)
+    fill(p("F1", 2, 72, 3, "F1o"), 0.0)
+    cp(p("F1", 1, 72, 3, "F1c"), p("xf", 0, 24))
+    op("g", lambda: g.affine_select(p("iotaj")[0], p("iotaj")[0], [[-1, CV]], A.is_gt, -1.0, C, 0), [p("iotaj")], [p("iotaj")])
+    targets(0)
+    halves(0)
 
     for t in (1, 2):
         merge(t)
-        quant_x(t)
-        planes(t, "s", (0, 1, 2))
-        scores(t)
+        planes(t, "g", (0, 1))
+        planes(t, "s", (2, 3))
+        for h in range(2):
+            quant_x(t, h)
+            scores(t, h)
         scores_late(t)
-        planes(t, "v", (3,))
-        if t == 1:
-            quant(p("vq"), p("vs"), p("VT"))
-        rise(t)
+        rise(t, 0)
+        rise(t, 1)
         entries()
-        late(t)
-        runs_end()
-        gather_e(t, ((0, "s"), (2, "v"), (1, "s"), (3, "v")))
-        targets_row()
-        layer(t)
+        late()
+        runs_end(t)
+        gather_e(t, ((2, "s"), (0, "v"), (3, "s"), (1, "v")))
+        quant_e(t)
         signed()
-        relus(((0, "s"), (1, "v"), (2, "s"), (3, "v")))
-        older_unpacked(t)
-        quant_h(t)
-        send_codes(t)
-        targets(t)
-        send_targets(t)
         resolve(t)
-        resolve_late(t)
-        between(t)
-    act(p("OLr"), ix(p("iotaj", 0, 400, 1, ["iotaj", "iotajp"]), p("el")))
-    dma("y", [(T.ol[:, :], T.OLr[0:128:16, :])], "dol", ["OLr"], [])
+        fired(t)
+        older(t)
+        if t == 1:
+            last()
+        else:
+            quant(p("vq"), p("vs"), p("VT"))
+            act(p("OLr"), ix(p("iotaj"), p("el2")))
+            dma("y", [(T.ol[:, :], T.OLr[0:128:16, :])], "dol", ["OLr"], [])
+        targets(t)
+        halves(t)
 
     merge(3)
-    H = C // 2
-    for h, bank in enumerate(("py", "py2")):
+    for h in range(2):
         a, e = H * h, H * h + H
-        quant(p("xq3", a, e, 1, "xq3%d" % h), p("xs3", a, e, 1, "xs3%d" % h), p("XT3", 4 * a, 4 * e, 1, XT(3)[1]))
-        mm(p(bank, 0, H), p("vq"), p("vs"), p("xq3", a, e, 1, "xq3%d" % h), p("xs3", a, e, 1, "xs3%d" % h))
-        dma("y", [(T.oc[:, 4 * a:4 * e], T.xq3[:, a:e].bitcast(dt.uint8))], "doc%d" % h, ["xq3%d" % h], [])
-    act(p("YT", 0, H, 1, "YT0"), p("py", 0, H))
-    cp(p("YT", H, C, 1, "YT1"), p("py2", 0, H))
+        quant_x(3, h)
+        mm(p(BANK[h], 0, H), p("vq"), p("vs"), *xq(3, h))
+        dma("y", [(T.oc[:, 4 * a:4 * e], T.xq3[:, a:e].bitcast(dt.uint8))], "doc%d" % h, ["xq3_%d" % h], [])
+    act(p("YT", 0, H, 1, "YT0"), p("psa", 0, H))
+    cp(p("YT", H, C, 1, "YT1"), p("psb", 0, H))
     dma("s", [(T.y[:, 0:H], T.YT[:, 0:H])], "dy0", ["YT0"], [])
-    dma("y", [(T.osc[4 * k:4 * k + 4, :], T.xs3[32 * k:32 * k + 4, :]) for k in range(4)], "dos", ["xs30", "xs31"], [])
+    dma("y", [(T.osc[4 * k:4 * k + 4, :], T.xs3[32 * k:32 * k + 4, :]) for k in range(4)], "dos", ["xs3_0", "xs3_1"], [])
     dma("y", [(T.y[:, H:C], T.YT[:, H:C])], "dy1", ["YT1"], [])
     for sem in sorted(total):
         if waited.get(sem, 0) < total[sem]:

@@ -2,14 +2,15 @@ from concourse.bass import DstId, RemoteDMATransfer
 from concourse.mybir import dt, AluOpType as A, ActivationFunctionType as F
 
 C, K, N = 384, 160, 8
-HALF = K // 2
+THIRD = 54
 H = C // 2
 CV = C + 16
 CS = C + 32
 MID = 208
 NZ = 4 * C + 4
-M1, V1, WEND = 400, 560, 1360
+M1, V1, WEND = C + 1, C + 1 + K, 1360
 LT = 10
+BIG = 8192.0
 R1 = 1.5 * 2.0 ** 23
 F32, BF, I32, U16, COD, U8 = "float32", "bfloat16", "int32", "uint16", "float8_e4m3fn_x4", "uint8"
 SCRATCH = {}
@@ -22,41 +23,40 @@ def _b(name, n, d, where="sbuf"):
 for _t in range(4):
     _b("XT%d" % _t, 4 * C, BF)
     _b("xq%d" % _t, C, COD)
-    _b("xs%d" % _t, C, U8)
+    _b("xs%d" % _t, C + K, U8)
     _b("ebq%d" % _t, 128, COD)
     _b("ebs%d" % _t, 128, U8)
     _b("XG%d" % _t, K, BF)
     _b("XD%d" % _t, K, BF)
-    _b("WB%d" % _t, WEND, BF)
 for _t in range(3):
-    for _n, _w, _d in [("eq", K, COD), ("es", K, U8), ("ql", K, COD), ("qls", K, U8), ("hq", K, COD), ("hs", K, U8), ("wm", 64, BF),
-                       ("le", LT, U16), ("lw", 64, BF), ("rc", HALF, COD), ("rs", K, U8), ("rt", LT, U16), ("rw", 64, BF)]:
+    for _n, _w, _d in [("eq", K, COD), ("ql", K, COD), ("qls", K, U8), ("hq", K, COD), ("hs", K, U8), ("wm", 64, BF),
+                       ("le", LT, U16), ("lw", 64, BF), ("rc", THIRD, COD), ("rs", 4 * THIRD, U8), ("rt", LT, U16), ("rw", 64, BF)]:
         _b("%s%d" % (_n, _t), _w, _d)
 for _n, _w, _d in [
-        ("UT", 512, BF), ("VT", 512, BF), ("uq", 128, COD), ("us", 128, U8), ("ur", 128, COD), ("urs", 128, U8),
-        ("ul", 128, COD), ("uls", 128, U8), ("vq", 128, COD), ("vs", 128, U8), ("wq", 512, COD), ("wsp", 512, U8),
+        ("UT", 512, BF), ("VT", 512, BF), ("uq", 128, COD), ("us", 128, U8), ("ur", 256, COD), ("urs", 256, U8),
+        ("vq", 128, COD), ("vs", 128, U8), ("wq", 512, COD), ("wsp", 512, U8),
         ("rwq", 128, COD), ("rws", 128, U8), ("wl", 512, COD), ("wls", 512, U8), ("rtg", 24, U16), ("tgp", 24, U16),
-        ("tgT", 24, I32), ("lanep", 1, I32), ("lanei", 1, I32), ("half", 576, BF),
-        ("EBW", 516, BF), ("vi", 24, I32), ("ET", 4 * K, BF), ("HT", 4 * K, BF), ("OLr", K, F32), ("YT", C, F32)]:
+        ("tgT", 24, I32), ("lanep", 1, I32), ("lanei", 1, I32),
+        ("EBW", 516, BF), ("vi", 48, I32), ("WB", 4 * WEND, BF), ("ET", 4 * K, BF), ("HT", 4 * K, BF), ("OLr", K, F32), ("YT", C, F32)]:
     _b(_n, _w, _d)
 PLACE, _end = {}, {}
 for _n, _w, _d in [
         ("lane", 1, F32), ("vini", 1, F32), ("thr", 1, F32),
-        ("x36", 36, F32), ("xf", 36, F32), ("q1", 36, F32), ("fl", 36, F32), ("q2", 36, F32), ("q3", 36, F32),
-        ("q4", 36, F32), ("q5", 36, F32), ("q6", 36, F32), ("RL", 36, U16), ("PL", 36, U16), ("KC", 576, BF), ("i16", CS, BF),
-        ("xio", CV, F32), ("I32", CV, F32), ("iotaj", CV, F32), ("Lr", 16, F32), ("D2", CS, BF), ("own", 16, BF),
-        ("pw", 16, F32), ("nr24", 576, BF), ("nr16", 32, F32), ("ones32", 32, F32), ("lu", 8, U16), ("ll", 8, U16),
-        ("zr", CV, BF), ("DR", CV, BF), ("tgu", 24, U16), ("OH", 576, BF), ("C1", 576, BF), ("Hh", 32, F32), ("HT1", 32, F32), ("PI", 32, F32), ("G1", 64, F32),
+        ("x36", 36, F32), ("r48", 36, F32), ("xf", 36, F32), ("q1", 36, F32), ("fl", 36, F32), ("q3", 36, F32),
+        ("q4", 36, F32), ("q6", 36, F32), ("hlf", 16, BF), ("RL", 36, U16), ("PL", 36, U16), ("KC", 576, BF), ("l26", 26, U16),
+        ("xio", CS, F32), ("I32", CV, BF), ("iotaj", C + 1, F32), ("D2", CS, BF), ("own", 16, BF),
+        ("pw", 16, F32), ("nr24", 608, BF), ("nr16", 32, F32), ("lu", 16, U16),
+        ("tgu", 24, U16), ("OH", 576, BF), ("C1", 576, BF), ("Hh", 32, F32), ("HT1", 32, F32), ("PI", 32, F32), ("G1", 64, F32),
         ("GT", 64, F32), ("BI", 33, F32), ("G2", 24, F32), ("C2", 576, BF), ("C2m", 576, BF), ("NOm", 576, BF),
-        ("SEL", 576, BF), ("rk", 24, U16), ("pir", CS, F32), ("pis", CS, F32), ("pia", 14, U16), ("pib", 12, U16), ("bx", 32, F32), ("be", 32, F32),
-        ("endl", 2, U16), ("tgx", CV, F32), ("NS", CS, BF),
-        ("P0", 1600, BF), ("P1", 1600, BF), ("Z", 1600, BF), ("RQ", CV, BF), ("ST", CV, F32),
-        ("ac1", 1, F32), ("al", 1, U16), ("TA", 16, F32), ("FF", 16, F32), ("el0", LT, U16), ("el1", LT, U16), ("el2", LT, U16),
+        ("SEL", 576, BF), ("rk", 26, U16), ("pir", CS, F32), ("pis", CS, F32), ("pia", 14, U16), ("pib", 12, U16), ("bx", 32, F32), ("be", 32, F32),
+        ("tgx", C + 1, F32), ("NS", CS, BF),
+        ("P0", 1600, BF), ("P1", 1600, BF), ("Z", 1600, BF), ("RQ", CV + 1, BF), ("DQ", CV, BF), ("ST", CV + 1, BF),
+        ("ac1", 1, F32), ("al", 1, U16), ("el0", 16, U16), ("el1", 16, U16), ("el2", 16, U16),
         ("lt0", LT, U16), ("lt1", LT, U16), ("lt2", LT, U16),
         ("ZS", CS, BF), ("SD1", CS + 1, BF), ("SD2", CS + 1, BF), ("LAST", C, F32), ("junk1", CV, BF),
-        ("TT", K, F32), ("TS", K, F32), ("FX", C, BF), ("FS", C, BF), ("DA", C, BF), ("thr2", 1, F32), ("fl24", 24, F32), ("fvV", 24, F32),
-        ("F0", 72, F32), ("F1", 72, F32), ("FQ", 72, F32), ("h2", 24, F32), ("e0", 24, F32),
-        ("e1", 24, F32), ("fin", 24, U16)]:
+        ("TT", K, F32), ("TS", K, F32), ("FS", C, BF), ("DA", C, BF), ("thr2", 1, F32), ("sg", 24, F32),
+        ("nxf", 24, F32), ("nx2", 16, F32), ("PA", 16, BF), ("F0", 96, F32), ("F1", 96, F32), ("G0s", 72, F32), ("G1s", 72, F32),
+        ("FQ", 96, F32), ("GQ", 72, F32), ("fin", 24, U16)]:
     PLACE[_n] = ("pack_" + _d, _end.get(_d, 0), _w)
     _end[_d] = _end.get(_d, 0) + (_w + 31) // 32 * 32
 for _d in _end:
@@ -66,7 +66,7 @@ for _n in PSUM:
     _b(_n, 512, F32, "psum")
 
 SEMAPHORES = (["cv", "cs", "ct", "cg", "dxa", "dxb", "du", "dtg", "dwc", "dws", "dv", "dol", "doc0", "doc1", "dos", "dy0", "dy1", "ls", "ro",
-               "dz", "rg", "rq", "rp", "lg", "lq"]
+               "rg", "rq", "rp", "lg", "lq"]
               + ["%s%d" % (_s, _t) for _s in ("la", "lb", "lm", "ha", "rl", "rb", "rm", "rh") for _t in range(3)])
 
 
@@ -102,15 +102,15 @@ def _relay_program(g, core, role, src, dst, T, topo):
         if role == 3:
             g.wait_ge(T.sem["rb%d" % t], n_all)
             fwd(T["le%d" % t][:, 0:LT], T["rt%d" % t][:, 0:LT], "lb%d" % t)
+            g.wait_ge(T.sem["rh%d" % t], n_all // 4)
+            fwd(T["qls%d" % t][:, 0:K], T["rs%d" % t][:, 4 * THIRD - K:4 * THIRD], "ha%d" % t)
             for at, a, b in ((0, "rl", "la"), (32, "rm", "lm"))[:2 if t < 2 else 1]:
                 g.wait_ge(T.sem["%s%d" % (a, t)], n_all)
                 fwd(T["lw%d" % t][:, at:at + 24], T["rw%d" % t][:, at:at + 24], "%s%d" % (b, t))
-        elif role == 2:
-            g.wait_ge(T.sem["rh%d" % t], n_all)
-            fwd(T["qls%d" % t][:, 0:K], T["rs%d" % t][:, 0:K], "ha%d" % t)
         else:
-            g.wait_ge(T.sem["rh%d" % t], n_all // 2)
-            fwd(T["ql%d" % t][:, HALF * role:HALF * role + HALF].bitcast(dt.uint8), T["rc%d" % t][:, 0:HALF].bitcast(dt.uint8), "ha%d" % t)
+            a, e = THIRD * role, min(THIRD * role + THIRD, K)
+            g.wait_ge(T.sem["rh%d" % t], n_all // 4)
+            fwd(T["ql%d" % t][:, a:e].bitcast(dt.uint8), T["rc%d" % t][:, THIRD - (e - a):THIRD].bitcast(dt.uint8), "ha%d" % t)
     g.wait_ge(T.sem.ro, sent[0])
 
 
@@ -205,15 +205,18 @@ def rank_program(g, core, T, topo):
 
     def sfill(out, n, c):
         if c:
-            act(out, p("half", 0, n), F.Identity, scale=0.0, bias=c)
+            act(out, p("nr24", 0, n), F.Identity, scale=0.0, bias=c)
         else:
-            act(out, p("half", 0, n), scale=0.0)
+            act(out, p("nr24", 0, n), scale=0.0)
 
     def signs(junk, in_, bias, accum):
         op("s", lambda: s.activation(junk[0], in_[0], F.Sign, bias=bias[0], accum_out=accum[0], scale=-1.0), [junk, accum], [in_, bias])
 
     def copy(q, out, in_):
         (cp if q == "v" else act)(out, in_)
+
+    def gcopy(out, in_, n):
+        op("g", lambda: g.affine_select(out[0], in_[0], [[0, n]], A.is_equal, 0.0, 0, 0), [out], [in_])
 
     def scaled(q, out, in_, c):
         if q == "s":
@@ -246,7 +249,7 @@ def rank_program(g, core, T, topo):
         return [p("%s%d" % (n, t), a, e, 1, ["%s%d_%d" % (n, t, i) for i in hs]) for n in ("xq", "xs")]
 
     def WB(b, a, e, parts):
-        return p("WB%d" % b, a, e, 1, ["W%s_%d" % (k, b) for k in parts])
+        return p("WB", WEND * b + a, WEND * b + e, 1, ["W%s_%d" % (k, b) for k in parts])
 
     BANK = ("psa", "psb")
 
@@ -255,17 +258,16 @@ def rank_program(g, core, T, topo):
 
     def planes(t, q, bs):
         for b in bs:
-            o, i = WB(b, 0, C, "X"), XT(t, b)
             if q == "g":
-                op("g", lambda: g.affine_select(o[0], i[0], [[0, C]], A.is_equal, 0.0, 0, 0), [o], [i])
+                gcopy(WB(b, 0, C, "X"), XT(t, b), C)
             else:
-                copy(q, o, i)
+                copy(q, WB(b, 0, C, "X"), XT(t, b))
 
     def scores(t, h):
-        mm(p(BANK[h], 0, H), p("ur"), p("urs"), *xq(t, h))
+        mm(p(BANK[h], 0, H), p("ur", 0, 128), p("urs", 0, 128), *xq(t, h))
 
     def scores_late(t):
-        mm(p("psl", 0, C), p("ul"), p("uls"), *xq(t))
+        mm(p("psl", 0, C), p("ur", 128, 256), p("urs", 128, 256), *xq(t))
 
     def rise(t, h):
         o = p("P0", 4 * H * h + 1, 4 * H * h + 4 * H, 4, "P0r%d" % h)
@@ -276,45 +278,54 @@ def rank_program(g, core, T, topo):
 
     FLAGS = ["P0", "P0r0", "P0r1", "P0v"]
 
-    def entries():
-        flags = p("P0", 1, 4 * CV, 4, FLAGS)
-        scan(p("P1", 0, 4 * CV, 4, "P1y"), flags, (p("zr", 0, CV)[0], ["zr", "P1"]), -161.0, A.add, A.min)
-        signs(p("junk1", 0, CV - 1), p("P1", 0, 4 * CV - 4, 4, "P1y"), p("thr"), p("ac1"))
-        scan(p("RQ"), flags, p("zr", 0, CV), p("vini"), A.add, A.add)
-        scan(p("ST"), p("DR"), p("RQ"), 0.0, A.add, A.max)
+    def entries(beside=(lambda: None,) * 3):
+        flags, y = p("P0", 1, 4 * CV, 4, FLAGS), p("P1", 0, 4 * CV, 4, "P1y")
+        zeros = p("P1", 1, 4 * CV, 4, "P11")
+        scan(y, flags, zeros, -161.0, A.add, A.min)
+        signs(p("junk1"), y, p("thr"), p("ac1"))
+        beside[0]()
+        scan(p("RQ", 1, CV + 1), flags, zeros, p("vini"), A.add, A.add)
+        beside[1]()
+        scan(p("DQ"), p("RQ", 1, CV + 1), p("RQ", 0, CV, 1, ["RQ", "RQ0"]), 0.0, A.max, A.subtract)
+        beside[2]()
+        scan(p("ST", 0, CV), p("DQ"), p("I32"), -8.0, A.add, A.min)
 
     def runs_end(t):
-        ts(p("al"), p("ac1"), float(CV - 1), A.add, 0.5, A.mult)
-        tt(p("TA"), ix(p("ST"), p("al")), p("Lr"), A.subtract)
-        tt(p("FF"), ix(p("I32"), p("al")), p("TA"), A.subtract)
-        ts(p("el%d" % t), p("FF", 0, LT), 32.0, A.mult, float(CV - 1), A.min)
-        send_list(p("el%d" % t), T["rt%d" % t][:, 0:LT], "rb%d" % t)
+        ts(p("al"), p("ac1"), float(CV), A.add, 0.5, A.mult)
+        ts(p("el%d" % t), ix(p("ST", key=["ST", "STz"]), p("al")), 32.0, A.mult, 200.0, A.add)
+        send_list(p("el%d" % t, 0, LT), T["rt%d" % t][:, 0:LT], "rb%d" % t)
 
     def late():
         o = p("P0", 2, 4 * C, 4, "P0l")
         op("s", lambda: s.activation(o[0], p("psl", 0, C)[0], F.Sign, bias=-2.0 ** -118), [o], [p("psl")])
 
     def signed():
-        scan(p("Z", 0, NZ), p("P0", 0, NZ, 1, FLAGS + ["P0l", "P0m", "P0z"]), p("P1", 0, NZ, 1, ["P1", "P1y"]), 0.0, A.mult, A.add)
+        scan(p("Z", 0, NZ), p("P0", 0, NZ, 1, FLAGS + ["P0l", "P0m", "P0z"]), p("P1", 0, NZ, 1, ["P1y", "P11", "P12", "P13"]), 0.0, A.mult, A.add)
+
+    ends = p("rk", 24, 26, 1, "endl")
 
     def resolve(t):
         act(p("ZS", 224, CS, 1, "ZSb"), ix(p("Z", 0, NZ), p("pib")))
         cp(p("ZS", 0, 224, 1, "ZSa"), ix(p("Z", 0, NZ), p("pia")))
+        if t:
+            older_halves(t, (2, 3))
+        else:
+            act(p("tgx", 0, C), ix(p("xio", 0, C), p("tgp")), F.Identity, scale=0.25, bias=2048.0 - 2051.0 / 4)
         zs = p("ZS", key=["ZSa", "ZSb"])
         scan(p("SD1", 1, CS + 1), p("NS"), zs, 0.0, A.mult, A.max)
-        cp(p("wm%d" % t, 0, 32, 1, "wm%da" % t), ix(p("SD1", 0, CS, 1, ["SD1", "SD10"]), p("endl")))
+        cp(p("wm%d" % t, 0, 32, 1, "wm%da" % t), ix(p("SD1", 0, CS, 1, ["SD1", "SD10"]), ends))
         send_list(p("wm%d" % t, 0, 24, 1, "wm%da" % t), T["rw%d" % t][:, 0:24], "rl%d" % t)
         if t < 2:
             scan(p("SD2", 1, CS + 1), p("NS"), zs, 0.0, A.mult, A.min)
-            ts(p("wm%d" % t, 32, 64, 1, "wm%db" % t), ix(p("SD2", 0, CS, 1, ["SD2", "SD20"]), p("endl")), -1.0, A.mult)
+            act(p("wm%d" % t, 32, 64, 1, "wm%db" % t), ix(p("SD2", 0, CS, 1, ["SD2", "SD20"]), ends), scale=-1.0)
             send_list(p("wm%d" % t, 32, 56, 1, "wm%db" % t), T["rw%d" % t][:, 32:56], "rm%d" % t)
 
     def gather_e(t, pairs):
         for b, q in pairs:
-            copy(q, p("ET", b, None, 4, "ET%d" % b), ix(WB(b, 0, M1, "X0"), p("el%d" % t)))
+            copy(q, p("ET", b, None, 4, "ET%d" % b), ix(WB(b, 0, M1, "X0"), p("el%d" % t, 0, LT)))
 
     def quant_e(t):
-        quant(p("eq%d" % t), p("es%d" % t), p("ET", 0, None, 1, ["ET%d" % b for b in range(4)]))
+        quant(p("eq%d" % t), p("xs%d" % t, C, C + K, 1, "es%d" % t), p("ET", 0, None, 1, ["ET%d" % b for b in range(4)]))
         send_codes(t)
 
     rel = _relays(rank, T, topo)
@@ -324,19 +335,20 @@ def rank_program(g, core, T, topo):
         g.remote_dma(out, in_, T.sem[sem], T.sem.ls, pid, rid, topo.mask(core, rel[i]))
         total["ls"] = total.get("ls", 0) + len(topo.engines(core, rel[i]))
 
-    def share(srcs, dst, sem):
+    def share(srcs, dsts, sem):
         es = topo.engines(core, rel[0])
         h, tr = len(es) // len(srcs), []
-        for i, src in enumerate(srcs):
+        for i, (src, dst) in enumerate(zip(srcs, dsts)):
             rid, pid = topo.addr(rel[i], core)
             tr.append(RemoteDMATransfer(dst_ids=[DstId(rid=rid, pnc=pid)], dma_engine_mask=_bits(es[h * i:h * i + h]), remote_sem=T.sem[sem], src=src, dst=dst))
         g.remote_dma_fused(tr, local_sem=T.sem.ls)
         total["ls"] = total.get("ls", 0) + len(es)
 
     def send_codes(t):
-        deps("g", ["eq%d" % t, "es%d" % t], [])
-        share([T["eq%d" % t][:, HALF * i:HALF * i + HALF].bitcast(dt.uint8) for i in range(2)], T["rc%d" % t][:, 0:HALF].bitcast(dt.uint8), "rh%d" % t)
-        send(2, T["rs%d" % t][:, 0:K], T["es%d" % t][:, 0:K], "rh%d" % t)
+        deps("g", ["eq%d" % t, "es%d" % t, "xs%d_1" % t], [])
+        ends = [min(THIRD * i + THIRD, K) for i in range(3)]
+        share([T["eq%d" % t][:, e - THIRD:e].bitcast(dt.uint8) for e in ends] + [T["xs%d" % t][:, C + K - 4 * THIRD:C + K]],
+              [T["rc%d" % t][:, 0:THIRD].bitcast(dt.uint8)] * 3 + [T["rs%d" % t][:, 0:4 * THIRD]], "rh%d" % t)
 
     def send_list(src, dst, sem):
         deps("g", src[1], [])
@@ -346,27 +358,34 @@ def rank_program(g, core, T, topo):
         for b in range(4):
             mm(p("pw%d" % b, 0, K), p("ebq%d" % b), p("ebs%d" % b), p("hq%d" % t), p("hs%d" % t))
 
-    def fired(t):
-        act(p("FX"), p("Z", 1, 4 * C, 4), F.Sign, scale=-1.0)
-        scan(p("FS"), p("DA"), p("FX"), 0.0, A.add, A.max)
-        ts(p("fl24"), p("FS", 15, C, 16), p("thr2"), A.is_gt, 160.0, A.mult)
-        ts(p("fvV"), p("fl24"), float(V1 + 320 * t), A.add)
-        if t >= 1:
-            was = p("lw%d" % (t - 1), 32, 56, 1, "lx%d" % (t - 1))
-            ts(p("e0"), p("fl24"), float(V1 + 320 * (t - 1)), A.add)
-            ts(p("h2"), was, 0.0, A.is_gt)
-            tt(p("e1"), p("e0"), was, A.subtract)
-            ts(p("F0", 2, 72, 3, "F0o"), was, 0.0, A.is_le)
-            tt(p("F1", 2, 72, 3, "F1o"), p("e1"), p("h2"), A.mult)
+    def fired():
+        scan(p("FS"), p("DA"), p("Z", 1, 4 * C, 4), 0.0, A.add, A.min)
 
-    def last():
-        for h in range(2):
+    def ends_of(t):
+        op("s", lambda: s.activation(p("sg")[0], p("FS", 15, C, 16)[0], F.Sign, bias=p("thr2")[0]), [p("sg")], [p("FS"), p("thr2")])
+        act(p("F1", 0, 96, 4, "F1d"), p("sg"), F.Identity, scale=80.0, bias=-80.0 - V1 - 320 * t)
+        if t >= 1:
+            act(p("G1s", 0, 72, 3, "G1d"), p("sg"), F.Identity, scale=80.0, bias=-80.0 - V1 - 320 * (t - 1))
+
+    def older_winners(t):
+        was = p("lw%d" % (t - 1), 32, 56, 1, "lx%d" % (t - 1))
+        act(p("G0s", 1, 72, 3, "G0w"), was)
+        act(p("G0s", 2, 72, 3, "G0n"), was, F.Relu, scale=-BIG, bias=BIG)
+        act(p("F0", 2, 96, 4, "F0o"), was, scale=BIG)
+
+    def older_places():
+        scan(p("GQ"), p("G0s", key=["FG", "G0w", "G0n"]), p("G1s", key=["FG", "G1d", "G1c"]), 0.0, A.add, A.min)
+        act(p("F1", 3, 96, 4, "F1r"), p("GQ", 2, 72, 3))
+
+    def last(hs):
+        for h in hs:
             act(p("LAST", H * h, H * h + H, 1, "LAST%d" % h), p(BANK[h], 0, H))
 
-    def older(t):
-        unpack(t - 1)
-        for b in range(4):
+    def older_halves(t, bs):
+        for b in bs:
             act(p("XD%d" % b), ix(WB(b, 0, M1, ["X", "0"]), p("lt%d" % (t - 1))), scale=0.5)
+
+    def older_means(t):
         for b in range(4):
             tt(WB(b, V1 + 320 * (t - 1), V1 + 320 * (t - 1) + K, ["A%d" % (t - 1)]), p("pw%d" % b, 0, K), p("XD%d" % b), A.add)
 
@@ -375,8 +394,8 @@ def rank_program(g, core, T, topo):
         lane_scan(p("TS"), p("TT"), K)
         unlane(p("lt%d" % t), p("TS", 15, K, 16))
 
-    def halves(t):
-        for b, q in ((0, "v"), (1, "s"), (2, "v"), (3, "s")):
+    def halves(t, pairs):
+        for b, q in pairs:
             scaled(q, p("XG%d" % b), ix(WB(b, 0, M1, ["X", "0"]), p("lt%d" % t)), 0.5)
 
     def merge(n):
@@ -392,10 +411,18 @@ def rank_program(g, core, T, topo):
                 ts(o, i, 0.0, A.max, 0.03125, A.mult)
         quant(p("hq%d" % t), p("hs%d" % t), p("HT", 0, None, 1, ["HT%d" % b for b in range(4)]))
         unpack(t)
-        ts(p("F0", 1, 72, 3, "F0h"), lw, 0.0, A.is_gt)
-        tt(p("F1", 0, 72, 3, "F1d"), p("fvV"), lw, A.subtract)
-        scan(p("FQ"), p("F0", key=["F0", "F0h", "F0o"]), p("F1", key=["F1d", "F1c", "F1o"]), 0.0, A.mult, A.max)
-        cp(p("fin"), p("FQ", 2, 72, 3))
+        if n == 1:
+            ends_of(0)
+
+        def winners():
+            act(p("F0", 1, 96, 4, "F0w"), lw)
+            act(p("F0", 3, 96, 4, "F0n"), lw, F.Relu, scale=-BIG, bias=BIG)
+
+        def places():
+            scan(p("FQ"), p("F0", key=["FG", "F0w", "F0o", "F0n"]), p("F1", key=["FG", "F1d", "F1r"]), 0.0, A.add, A.min)
+
+        def table():
+            ts(p("fin"), p("FQ", 3, 96, 4), -1.0, A.mult)
 
         def mean(b):
             tt(WB(b, a, a + K, ["A%d" % t]), p("pw%d" % b, 0, K), p("XG%d" % b), A.add)
@@ -403,13 +430,16 @@ def rank_program(g, core, T, topo):
         def move(b):
             act(WB(b, m, m + K, ["M%d" % t]), p("pw%d" % b, 0, K), scale=2.0)
 
-        mean(0), move(1), mean(2), move(3), mean(1), move(0), mean(3), move(2)
+        if n == 1:
+            mean(0), move(1), mean(2), move(3), winners(), mean(1), move(0), mean(3), places(), move(2), table()
+        else:
+            winners(), mean(0), move(1), mean(2), places(), move(3), mean(1), table(), move(0), mean(3), move(2)
         for b, q in ((0, "s"), (1, "v"), (2, "s"), (3, "v")):
             copy(q, XT(n, b), ix(WB(b, 0, a + K, ["X", "0"] + ["%s%d" % (k, i) for i in range(n) for k in "MA"]), p("fin")))
 
     arrivals = [("lg", 8, ["tgp"]), ("lq", 64, ["wl", "wls"])]
     for t in range(3):
-        arrivals += [("lb%d" % t, 8, ["le%d" % t]), ("la%d" % t, 8, ["lw%d" % t]), ("ha%d" % t, 24, ["ql%d" % t, "qls%d" % t])]
+        arrivals += [("lb%d" % t, 8, ["le%d" % t]), ("la%d" % t, 8, ["lw%d" % t]), ("ha%d" % t, 32, ["ql%d" % t, "qls%d" % t])]
         arrivals += [("lm%d" % t, 8, ["lx%d" % t])] if t < 2 else []
     for sem, n, keys in arrivals:
         total[sem] = n
@@ -420,134 +450,141 @@ def rank_program(g, core, T, topo):
     dma("s", [(T.XT0[:, 0:4 * H], T.x[:, 0:4 * H])], "dxa", [], XT(0, None, 0)[1])
     dma("y", [(T.XT0[:, 4 * H:4 * C], T.x[:, 4 * H:4 * C])], "dxb", [], XT(0, None, 1)[1])
 
-    fill(p("half"), 0.5)
-    fill(p("zr"), 0.0)
+    fill(p("nr24"), 1.0)
+    nr24, ones32 = p("nr24", 0, 576), p("nr24", 576, 608)
     iota(p("lanep"), [[1, 1]], 0, 1)
     iota(p("x36"), [[16, 36]])
+    iota(p("r48"), [[0, 12], [16, 3]])
     iota(p("KC"), [[1, 24], [0, 24]])
-    iota(p("i16"), [[0, 26], [1, 16]])
-    dma("y", [(T.pack_bfloat16[:, PLACE["P1"][1] + 400 * i:PLACE["P1"][1] + 400 * i + 400], p("zr", 0, 400)[0]) for i in range(4)], "dz", ["zr"], ["P1"])
     dma("y", [(T.wsp[:, :], T.ws[:, :])], "dws", [], ["wsp"])
     dma("y", [(T.wq[:, :].bitcast(dt.uint8), T.wc[:, :])], "dwc", [], ["wq"])
-    sfill(p("nr24"), 576, 1.0)
-    sfill(p("nr24", 0, 576, 24), 24, 0.0)
+
+    def affine(out, in_, a, b):
+        act(out, in_, F.Identity, scale=a, bias=b)
+
+    ts(p("lanei"), p("lanep"), 15, A.bitwise_and)
+    fill(p("nr24", 0, 576, 24), 0.0)
+    cp(p("lane"), p("lanei"))
+    cp(p("lu", 0, 8), p("x36", 0, 8))
+    ts(p("xf"), p("x36"), p("lane"), A.add)
+    ts(p("lu", 8, 16, 1, "ll"), p("x36", 0, 8), 1.0, A.add)
+    ts(p("RL"), p("r48"), p("lane"), A.add)
+    ts(p("own"), p("x36", 0, 16), 1.0 / 16, A.mult, p("lane"), A.is_equal)
+    ts(p("l26"), p("x36", 0, 26), 0.0, A.mult, p("lane"), A.add)
+    fill(p("nx2", 0, 1, 1, "nx0"), 0.0)
+    ts(p("nx2", 1, 16), p("own", 0, 15), -255.0 / 1024, A.mult)
+    ts(p("nxf"), p("xf", 0, 24), -1.0, A.mult)
     sfill(p("Hh"), 32, 0.0)
+    sfill(p("hlf"), 16, 0.5)
     sfill(p("nr16"), 32, 1.0)
-    sfill(p("ones32"), 32, 1.0)
+    affine(p("q1"), p("xf"), 1.0 / 24, -11.5 / 24)
     sfill(p("nr16", 0, 32, 16), 2, 0.0)
+    affine(p("q3"), p("xf"), -24.0, 552.0)
+    ts(p("fl"), p("q1"), R1, A.add, R1, A.subtract)
+    scan(p("pw"), p("hlf"), p("own"), 0.0, A.mult, A.max)
+    tt(p("PA"), p("nx2", key=["nx2", "nx0"]), p("own"), A.add)
+    ts(p("thr2"), p("own", 15, 16), -255.0, A.mult, 255.5, A.add)
+    affine(p("q4"), p("fl"), 577.0, 0.0)
+    act(p("D2"), ix(p("own"), p("l26")), F.Identity, scale=-2.0, bias=2.0)
+    affine(p("vini"), p("lane"), -1.0, 2064.0 + 7.5)
+    affine(p("thr"), p("lane"), 16.0, -145.5)
     sfill(p("BI", 0, 1, 1, "BI0"), 1, -1.0 - MID)
     sfill(p("P0", 0, NZ, 4, "P0"), C + 1, 0.0)
     sfill(p("P0", 4 * C + 2, 4 * C + 4, 1, "P0z"), 2, 0.0)
     sfill(p("P0", 4 * C + 1, 4 * CV, 4, "P0v"), 16, 1.0)
-    sfill(p("DR"), CV, 1.0 / 32)
-    for b in range(4):
-        sfill(WB(b, C, M1, "0"), 16, 0.0)
-    sfill(p("pir"), CS, 2048.0 + 4 * C + 3)
-    sfill(p("NS"), CS, 1.0)
-
-    ts(p("lanei"), p("lanep"), 15, A.bitwise_and)
-    cp(p("lu"), p("x36", 0, 8))
-    cp(p("lane"), p("lanei"))
-    ts(p("ll"), p("x36", 0, 8), 1.0, A.add)
-    ts(p("xf"), p("x36"), p("lane"), A.add)
-    ts(p("Lr"), p("x36", 0, 16), 2080.0, A.add)
-    ts(p("q1"), p("xf"), 1.0 / 24, A.mult, -11.5 / 24, A.add)
-    ts(p("q3"), p("xf"), -24.0, A.mult, 552.0, A.add)
-    ts(p("fl"), p("q1"), R1, A.add, R1, A.subtract)
-    ts(p("vini"), p("lane"), -1.0, A.mult, 2064.0 + 7.5, A.add)
-    ts(p("q2"), p("fl"), -24.0, A.mult)
-    ts(p("q4"), p("fl"), 577.0, A.mult)
-    tt(p("q5"), p("q2"), p("xf"), A.add)
+    sfill(p("RQ", 0, 1, 1, "RQ0"), 1, 2064.0)
+    sfill(p("ST", CV, CV + 1, 1, "STz"), 1, (C - 200) / 32.0)
+    sfill(p("WB", C, None, WEND, ["W0_%d" % b for b in range(4)]), 4, 0.0)
     tt(p("q6"), p("q4"), p("q3"), A.add)
-    cp(p("RL"), p("q5"))
-    cp(p("PL"), p("q6"))
-    ts(p("thr"), p("lane"), 16.0, A.mult, -145.5, A.add)
-    ts(p("thr2"), p("lane"), -2.0, A.mult, 30.5, A.add)
+    sfill(p("P1", 1, 4 * CV, 4, "P11"), CV, 0.0)
 
-    ts(p("vi"), p("tgT"), 4, A.arith_shift_right)
-    cp(p("tgu"), p("tgT"))
-    send_list(p("tgu"), T.rtg[:, 0:24], "rg")
-    iota(p("xio"), [[4, CV]], 2048 + 3)
-    planes(0, "g", (0, 1))
-    deps("g", ["wsp"], [])
-    share([T.wsp[:, 128 * i:128 * i + 128] for i in range(4)], T.rws[:, 0:128], "rp")
-    planes(0, "g", (2,))
-    deps("g", ["wq"], [])
-    share([T.wq[:, 128 * i:128 * i + 128].bitcast(dt.uint8) for i in range(4)], T.rwq[:, 0:128].bitcast(dt.uint8), "rq")
-    planes(0, "g", (3,))
-    tt(p("OH"), ix(p("vi"), p("RL")), p("KC"), A.is_equal)
-    act(p("NOm"), ix(p("OH"), p("PL")), scale=-1000.0)
-    scan(p("C1"), p("nr24"), p("OH"), 0.0, A.mult, A.add)
-    ts(p("D2"), p("i16"), p("lane"), A.not_equal, 2.0, A.mult)
-    cp(p("Hh", 0, 24), p("C1", 23, 576, 24))
-    quant(p("uq"), p("us"), p("UT"))
-    turn(p("HT1"), p("Hh"))
-    act(p("urs"), ix(p("us"), p("lu")))
-    ts(p("own"), p("D2", 0, 16), -0.5, A.mult, 1.0, A.add)
-    scan(p("PI"), p("nr16"), p("HT1"), 0.0, A.mult, A.add)
-    scan(p("pw"), p("half", 0, 16), p("own"), 0.0, A.mult, A.max)
-    tt(p("G1", 0, 32), p("PI"), p("HT1"), A.subtract)
     for a in range(2):
-        ts(p("G1", 32 + 16 * a, 48 + 16 * a, 1, "G1%d" % a), p("ones32", 0, 16), p("PI", 16 * a + 15, 16 * a + 16), A.mult, 1.0, A.add)
-    cp(cast(p("ur"), dt.uint32), ix(cast(p("uq"), dt.uint32), p("lu")))
-    turn(p("GT"), p("G1", key=["G1", "G10", "G11"]))
+        ts(p("vi", 24 * a, 24 * a + 24, 1, "vi%d" % a), p("tgT"), 4, A.arith_shift_right)
+    cp(p("tgu"), p("tgT"))
+    cp(p("PL"), p("q6"))
+    send_list(p("tgu"), T.rtg[:, 0:24], "rg")
+    iota(p("xio", 0, C), [[4, C]], 2048 + 3)
+    iota(p("xio", C, CS, 1, "xioz"), [[0, CS - C]], 2048 + NZ - 1)
+    XIO = ["xio", "xioz"]
+    iota(p("P1", 2, NZ, 4, "P12"), [[0, C + 1]])
+    planes(0, "g", (0,))
+    deps("g", ["wsp"], [])
+    share([T.wsp[:, 128 * i:128 * i + 128] for i in range(4)], [T.rws[:, 0:128]] * 4, "rp")
+    deps("g", ["wq"], [])
+    share([T.wq[:, 128 * i:128 * i + 128].bitcast(dt.uint8) for i in range(4)], [T.rwq[:, 0:128].bitcast(dt.uint8)] * 4, "rq")
+    planes(0, "g", (1, 2))
+    tt(p("OH"), ix(p("vi", key=["vi0", "vi1"]), p("RL")), p("KC"), A.is_equal)
+    quant(p("uq"), p("us"), p("UT"))
+    scan(p("C1"), nr24, p("OH"), 0.0, A.mult, A.add)
+    lu = p("lu", key=["lu", "ll"])
+    act(p("urs"), ix(p("us"), lu))
+    act(p("NOm"), ix(p("OH"), p("PL")), scale=-1000.0)
+    cp(p("Hh", 0, 24), p("C1", 23, 576, 24))
+    cp(cast(p("ur"), dt.uint32), ix(cast(p("uq"), dt.uint32), lu))
+    turn(p("HT1"), p("Hh"))
     quant_x(0, 0)
     scores(0, 0)
-    scan(p("BI", 1, 33), p("ones32"), p("GT", 32, 64), -1.0 - MID, A.mult, A.add)
+    scan(p("PI"), p("nr16"), p("HT1"), 0.0, A.mult, A.add)
     quant_x(0, 1)
     scores(0, 1)
-    tt(p("G2"), p("GT", 0, 24), p("BI", 0, 24, 1, ["BI", "BI0"]), A.add)
-    ts(p("bx"), p("BI", 1, 33), 2048.0 + 1 + MID, A.add)
-    tt(p("OH", 0, 576, 24), p("OH", 0, 576, 24), p("G2"), A.add)
-    lane_scan(p("be"), p("bx"), 32)
-    scan(p("C2"), p("nr24"), p("OH"), 0.0, A.mult, A.add)
-    act(p("I32"), p("xio"), F.Identity, scale=1.0 / 128, bias=-2051.0 / 128)
-    act(p("C2m"), ix(p("C2"), p("PL")))
+    tt(p("G1", 0, 32), p("PI"), p("HT1"), A.subtract)
+    for a in range(2):
+        ts(p("G1", 32 + 16 * a, 48 + 16 * a, 1, "G1%d" % a), p("nr24", 576, 592), p("PI", 16 * a + 15, 16 * a + 16), A.mult, 1.0, A.add)
     rise(0, 0)
+    turn(p("GT"), p("G1", key=["G1", "G10", "G11"]))
     rise(0, 1)
-    entries()
-    cp(cast(p("ul"), dt.uint32), ix(cast(p("uq"), dt.uint32), p("ll")))
-    act(p("uls"), ix(p("us"), p("ll")))
-    act(p("P0", 3, 4 * C, 4, "P0m"), ix(p("D2", 0, C), p("tgu")), F.Identity, scale=-0.5, bias=1.0)
-    runs_end(0)
-    dma("y", [(T.VT[:, :], T.v[:, :])], "dv", ["el0"], ["VT"])
+    scan(p("BI", 1, 33), ones32, p("GT", 32, 64), -1.0 - MID, A.mult, A.add)
+    act(p("I32"), p("xio", 0, CV, 1, XIO), F.Identity, scale=1.0 / 128, bias=-2851.0 / 128)
     scores_late(0)
-    scan(p("SEL"), p("NOm"), p("C2m"), -2000.0, A.add, A.max)
-    unlane(p("endl"), p("be", 15, 32, 16), 1.0)
-    ts(p("rk"), p("SEL", 23, 576, 24), float(MID), A.add)
-    gather_e(0, ((0, "s"), (1, "s"), (2, "s"), (3, "s")))
     late()
-    cp(ix(p("pir"), p("rk")), p("xio", 0, C))
+    tt(p("G2"), p("GT", 0, 24), p("BI", 0, 24, 1, ["BI", "BI0"]), A.add)
+    entries((lambda: tt(p("OH", 0, 576, 24), p("OH", 0, 576, 24), p("G2"), A.add),
+             lambda: scan(p("C2"), nr24, p("OH"), 0.0, A.mult, A.add),
+             lambda: None))
+    act(p("C2m"), ix(p("C2"), p("PL")))
+    ts(p("bx"), p("BI", 1, 33), 2048.0 + 1 + MID, A.add)
+    planes(0, "s", (3,))
+    runs_end(0)
+    lane_scan(p("be"), p("bx"), 32)
+    unlane(ends, p("be", 15, 32, 16), 1.0)
+    iota(p("P1", 3, NZ, 4, "P13"), [[0, C + 1]])
+    op("g", lambda: g.affine_select(T.EBW[:, :], p("nr24", 0, 516)[0], [[1, 516]], A.is_equal, 0.0, -3, -4), [p("EBW")], [p("nr24")])
+    scan(p("SEL"), p("NOm"), p("C2m"), -2000.0, A.add, A.max)
+    ts(p("rk", 0, 24), p("SEL", 23, 576, 24), float(MID), A.add)
+    gather_e(0, ((0, "s"), (1, "s"), (2, "s"), (3, "s")))
+    act(p("P0", 3, 4 * C, 4, "P0m"), ix(p("D2", 0, C), p("tgu")), F.Identity, scale=-0.5, bias=1.0)
+    cp(ix(p("pir"), p("rk", key=["rk", "endl"])), p("xio", key=XIO))
+    act(p("NS"), p("pir"), F.Sign, scale=-1.0, bias=2048.0 + NZ - 1)
     quant_e(0)
-    op("g", lambda: g.affine_select(T.EBW[:, :], T.half[:, 0:516], [[1, 516]], A.is_equal, 0.0, -3, -4), [p("EBW")], [p("half")])
+    iota(p("F0", 0, 4 * 96, 1, "FG"), [[0, 4 * 96]], int(BIG))
+    iota(p("F0", 2, 96, 4, ["F0o", "FG"]), [[0, 24]])
+    for o in (p("F1", 3, 96, 4, ["F1r", "FG"]), p("G1s", 2, 72, 3, ["G1c", "FG"])):
+        gcopy(o, p("nxf"), 24)
+    iota(p("tgx", C, C + 1, 1, "tgxp"), [[1, 1]], 2048)
     lane_scan(p("pis"), p("pir"), CS)
-    cp(ix(p("NS"), p("endl")), p("zr", 0, 32))
     unlane(p("pib"), p("pis", 239, CS, 16))
     unlane(p("pia"), p("pis", 15, 224, 16))
     sfill(p("SD1", 0, 1, 1, "SD10"), 1, 0.0)
-    sfill(p("SD2", 0, 1, 1, "SD20"), 1, 0.0)
-    sfill(p("tgx", C, CV, 1, "tgxp"), 16, 2048.0)
-    act(p("DA"), p("D2", 0, C), F.Identity, scale=33.0, bias=-64.0)
+    act(p("EBW"), p("EBW"), scale=0.5)
     signed()
+    sfill(p("SD2", 0, 1, 1, "SD20"), 1, 0.0)
     resolve(0)
-    iota(p("iotaj"), [[1, CV]])
-    act(p("tgx", 0, C), ix(p("xio"), p("tgp")), F.Identity, scale=0.25, bias=2048.0 - 2051.0 / 4)
+    dma("y", [(T.VT[:, :], T.v[:, :])], "dv", ["wm0b"], ["VT"])
     for b in range(4):
         quant(p("ebq%d" % b), p("ebs%d" % b), p("EBW", 3 - b, 515 - b))
-    fired(0)
-    last()
-    fill(p("F0", 0, 72, 3), 0.0)
-    fill(p("F0", 2, 72, 3, "F0o"), 1.0)
-    fill(p("F1", 2, 72, 3, "F1o"), 0.0)
-    cp(p("F1", 1, 72, 3, "F1c"), p("xf", 0, 24))
-    op("g", lambda: g.affine_select(p("iotaj")[0], p("iotaj")[0], [[-1, CV]], A.is_gt, -1.0, C, 0), [p("iotaj")], [p("iotaj")])
     targets(0)
-    halves(0)
+    act(p("DA"), ix(p("PA"), p("l26", 0, 24)), scale=1024.0)
+    halves(0, ((0, "v"), (1, "s"), (2, "v"), (3, "s")))
+    fired()
+    iota(p("iotaj", 0, C), [[1, C]])
+    iota(p("iotaj", C, C + 1, 1, "iotajp"), [[1, 1]], -1)
 
     for t in (1, 2):
         merge(t)
-        planes(t, "g", (0, 1))
-        planes(t, "s", (2, 3))
+        if t == 1:
+            last((0, 1))
+        planes(t, "g", (0, 1, 2))
+        planes(t, "s", (3,))
         for h in range(2):
             quant_x(t, h)
             scores(t, h)
@@ -557,22 +594,26 @@ def rank_program(g, core, T, topo):
         entries()
         late()
         runs_end(t)
-        gather_e(t, ((2, "s"), (0, "v"), (3, "s"), (1, "v")))
+        gather_e(t, ((3, "s"), (0, "v"), (2, "s"), (1, "v")))
         quant_e(t)
+        if t == 1:
+            last((0, 1))
+        unpack(t - 1)
+        older_halves(t, (0, 1))
         signed()
         resolve(t)
-        fired(t)
-        older(t)
-        if t == 1:
-            last()
-        else:
-            quant(p("vq"), p("vs"), p("VT"))
-            act(p("OLr"), ix(p("iotaj"), p("el2")))
-            dma("y", [(T.ol[:, :], T.OLr[0:128:16, :])], "dol", ["OLr"], [])
+        fired()
+        ends_of(t)
+        older_means(t)
         targets(t)
-        halves(t)
+        older_winners(t)
+        older_places()
+        halves(t, ((0, "v"), (1, "s"), (2, "v"), (3, "s")))
+    quant(p("vq"), p("vs"), p("VT"))
 
     merge(3)
+    act(p("OLr"), ix(p("iotaj", key=["iotaj", "iotajp"]), p("el2", 0, LT)))
+    dma("y", [(T.ol[:, :], T.OLr[0:128:16, :])], "dol", ["OLr"], [])
     for h in range(2):
         a, e = H * h, H * h + H
         quant_x(3, h)
@@ -581,8 +622,8 @@ def rank_program(g, core, T, topo):
     act(p("YT", 0, H, 1, "YT0"), p("psa", 0, H))
     cp(p("YT", H, C, 1, "YT1"), p("psb", 0, H))
     dma("s", [(T.y[:, 0:H], T.YT[:, 0:H])], "dy0", ["YT0"], [])
-    dma("y", [(T.osc[4 * k:4 * k + 4, :], T.xs3[32 * k:32 * k + 4, :]) for k in range(4)], "dos", ["xs3_0", "xs3_1"], [])
-    dma("y", [(T.y[:, H:C], T.YT[:, H:C])], "dy1", ["YT1"], [])
+    dma("y", [(T.osc[4 * k:4 * k + 4, :], T.xs3[32 * k:32 * k + 4, 0:C]) for k in range(4)], "dos", ["xs3_0", "xs3_1"], [])
+    dma("s", [(T.y[:, H:C], T.YT[:, H:C])], "dy1", ["YT1"], [])
     for sem in sorted(total):
         if waited.get(sem, 0) < total[sem]:
             g.wait_ge(T.sem[sem], total[sem])

from concourse.bass import DstId, RemoteDMATransfer
from concourse.mybir import dt, AluOpType as A, ActivationFunctionType as F

C, K, N = 384, 160, 8
THIRD = 54
H = C // 2
CV = C + 16
CS = C + 32
MID = 208
NZ = 4 * C + 4
M1, V1, WEND = C + 1, C + 1 + K, 1360
LT = 10
BIG = 8192.0
R1 = 1.5 * 2.0 ** 23
F32, BF, I32, U16, COD, U8 = "float32", "bfloat16", "int32", "uint16", "float8_e4m3fn_x4", "uint8"
SCRATCH = {}


def _b(name, n, d, where="sbuf"):
    SCRATCH[name] = (where, [128, n], d)


for _t in range(4):
    _b("XT%d" % _t, 4 * C, BF)
    _b("xq%d" % _t, C, COD)
    _b("xs%d" % _t, C + K, U8)
    _b("ebq%d" % _t, 128, COD)
    _b("ebs%d" % _t, 128, U8)
    _b("XG%d" % _t, K, BF)
    _b("XD%d" % _t, K, BF)
for _t in range(3):
    for _n, _w, _d in [("eq", K, COD), ("ql", K, COD), ("qls", K, U8), ("hq", K, COD), ("hs", K, U8), ("wm", 64, BF),
                       ("le", LT, U16), ("lw", 64, BF), ("rc", THIRD, COD), ("rs", 4 * THIRD, U8), ("rt", LT, U16), ("rw", 64, BF)]:
        _b("%s%d" % (_n, _t), _w, _d)
for _n, _w, _d in [
        ("UT", 512, BF), ("VT", 512, BF), ("uq", 128, COD), ("us", 128, U8), ("ur", 256, COD), ("urs", 256, U8),
        ("vq", 128, COD), ("vs", 128, U8), ("wq", 512, COD), ("wsp", 512, U8),
        ("rwq", 128, COD), ("rws", 128, U8), ("wl", 512, COD), ("wls", 512, U8), ("rtg", 24, U16), ("tgp", 24, U16),
        ("tgT", 24, I32), ("lanep", 1, I32), ("lanei", 1, I32),
        ("EBW", 516, BF), ("vi", 48, I32), ("WB", 4 * WEND, BF), ("ET", 4 * K, BF), ("HT", 4 * K, BF), ("OLr", K, F32), ("YT", C, F32)]:
    _b(_n, _w, _d)
PLACE, _end = {}, {}
for _n, _w, _d in [
        ("lane", 1, F32), ("vini", 1, F32), ("thr", 1, F32),
        ("x36", 36, F32), ("r48", 36, F32), ("xf", 36, F32), ("q1", 36, F32), ("fl", 36, F32), ("q3", 36, F32),
        ("q4", 36, F32), ("q6", 36, F32), ("hlf", 16, BF), ("RL", 36, U16), ("PL", 36, U16), ("KC", 576, BF), ("l26", 26, U16),
        ("xio", CS, F32), ("I32", CV, BF), ("iotaj", C + 1, F32), ("D2", CS, BF), ("own", 16, BF),
        ("pw", 16, F32), ("nr24", 608, BF), ("nr16", 32, F32), ("lu", 16, U16),
        ("tgu", 24, U16), ("OH", 576, BF), ("C1", 576, BF), ("Hh", 32, F32), ("HT1", 32, F32), ("PI", 32, F32), ("G1", 64, F32),
        ("GT", 64, F32), ("BI", 33, F32), ("G2", 24, F32), ("C2", 576, BF), ("C2m", 576, BF), ("NOm", 576, BF),
        ("SEL", 576, BF), ("rk", 26, U16), ("pir", CS, F32), ("pis", CS, F32), ("pia", 14, U16), ("pib", 12, U16), ("bx", 32, F32), ("be", 32, F32),
        ("tgx", C + 1, F32), ("NS", CS, BF),
        ("P0", 1600, BF), ("P1", 1600, BF), ("Z", 1600, BF), ("RQ", CV + 1, BF), ("DQ", CV, BF), ("ST", CV + 1, BF),
        ("ac1", 1, F32), ("al", 1, U16), ("el0", 16, U16), ("el1", 16, U16), ("el2", 16, U16),
        ("lt0", LT, U16), ("lt1", LT, U16), ("lt2", LT, U16),
        ("ZS", CS, BF), ("SD1", CS + 1, BF), ("SD2", CS + 1, BF), ("LAST", C, F32), ("junk1", CV, BF),
        ("TT", K, F32), ("TS", K, F32), ("FS", C, BF), ("DA", C, BF), ("thr2", 1, F32), ("sg", 24, F32),
        ("nxf", 24, F32), ("nx2", 16, F32), ("PA", 16, BF), ("F0", 96, F32), ("F1", 96, F32), ("G0s", 72, F32), ("G1s", 72, F32),
        ("FQ", 96, F32), ("GQ", 72, F32), ("fin", 24, U16)]:
    PLACE[_n] = ("pack_" + _d, _end.get(_d, 0), _w)
    _end[_d] = _end.get(_d, 0) + (_w + 31) // 32 * 32
for _d in _end:
    _b("pack_" + _d, _end[_d], _d)
PSUM = ["pw0", "pw1", "pw2", "pw3", "psa", "psb", "psl"]
for _n in PSUM:
    _b(_n, 512, F32, "psum")

SEMAPHORES = (["cv", "cs", "ct", "cg", "dxa", "dxb", "du", "dtg", "dwc", "dws", "dv", "dol", "doc0", "doc1", "dos", "dy0", "dy1", "ls", "ro",
               "rg", "rq", "rp", "lg", "lq"]
              + ["%s%d" % (_s, _t) for _s in ("la", "lb", "lm", "ha", "rl", "rb", "rm", "rh") for _t in range(3)])


def _bits(es):
    return sum(1 << e for e in es)


def _relays(rank, T, topo):
    me, dst = T.cores[rank], T.cores[(rank + 1) % N]
    able = [c for c in topo.cores_of(me) if c != me and topo.may_write(c, dst)]
    near = [c for c in able if topo.die(c) == topo.die(me)]
    far = [c for c in able if topo.die(c) != topo.die(me)]
    return near[0], far[0], near[1], far[1]


def _relay_program(g, core, role, src, dst, T, topo):
    rid, pid = topo.addr(dst, core)
    mask, n_out, n_all = topo.mask(core, dst), len(topo.engines(core, dst)), len(topo.engines(src, core))
    sent = [0]

    def fwd(out, in_, sem):
        g.remote_dma(out, in_, T.sem[sem], T.sem.ro, pid, rid, mask)
        sent[0] += n_out

    if role == 3:
        g.wait_ge(T.sem.rg, n_all)
        fwd(T.tgp[:, 0:24], T.rtg[:, 0:24], "lg")
    g.wait_ge(T.sem.rp, n_all // 4)
    fwd(T.wls[:, 128 * role:128 * role + 128], T.rws[:, 0:128], "lq")
    g.wait_ge(T.sem.rq, n_all // 4)
    fwd(T.wl[:, 128 * role:128 * role + 128].bitcast(dt.uint8), T.rwq[:, 0:128].bitcast(dt.uint8), "lq")
    for t in range(3):
        if role == 3:
            g.wait_ge(T.sem["rb%d" % t], n_all)
            fwd(T["le%d" % t][:, 0:LT], T["rt%d" % t][:, 0:LT], "lb%d" % t)
            g.wait_ge(T.sem["rh%d" % t], n_all // 4)
            fwd(T["qls%d" % t][:, 0:K], T["rs%d" % t][:, 4 * THIRD - K:4 * THIRD], "ha%d" % t)
            for at, a, b in ((0, "rl", "la"), (32, "rm", "lm"))[:2 if t < 2 else 1]:
                g.wait_ge(T.sem["%s%d" % (a, t)], n_all)
                fwd(T["lw%d" % t][:, at:at + 24], T["rw%d" % t][:, at:at + 24], "%s%d" % (b, t))
        else:
            a, e = THIRD * role, min(THIRD * role + THIRD, K)
            g.wait_ge(T.sem["rh%d" % t], n_all // 4)
            fwd(T["ql%d" % t][:, a:e].bitcast(dt.uint8), T["rc%d" % t][:, THIRD - (e - a):THIRD].bitcast(dt.uint8), "ha%d" % t)
    g.wait_ge(T.sem.ro, sent[0])


def rank_program(g, core, T, topo):
    rank = T.rank_of(core)
    if rank is None:
        for r, c in enumerate(T.cores):
            if core in topo.cores_of(c):
                rel = _relays(r, T, topo)
                if core in rel:
                    _relay_program(g, core, rel.index(core), c, T.cores[(r + 1) % N], T, topo)
        return
    queue = {"v": g.vector, "s": g.scalar, "t": g.tensor, "g": g, "y": g.sync}
    own = {"v": "cv", "s": "cs", "t": "ct", "g": "cg"}
    total, waited, known = {}, {}, {q: {} for q in queue}
    writer, readers = {}, {}

    def deps(q, R, W):
        evs = [writer[k] for k in R if k in writer]
        for k in W:
            evs += readers.get(k, []) + ([writer[k]] if k in writer else [])
        for e in sorted(evs, key=lambda e: (-sum(e["clock"].values()), e["sem"])):
            if known[q].get(e["sem"], 0) < e["n"]:
                queue[q].wait_ge(T.sem[e["sem"]], e["n"])
                waited[e["sem"]] = max(waited.get(e["sem"], 0), e["n"])
                for s, n in e["clock"].items():
                    known[q][s] = max(known[q].get(s, 0), n)

    def note(sem, kq, R, W):
        clock = dict(known[kq]) if kq else {}
        clock[sem] = total[sem]
        ev = {"sem": sem, "n": total[sem], "clock": clock}
        for k in R:
            readers.setdefault(k, []).append(ev)
        for k in W:
            writer[k], readers[k] = ev, []

    def p(name, a=0, b=None, step=1, key=None):
        buf, at, w = PLACE[name] if name in PLACE else (name, 0, SCRATCH[name][1][1])
        return T[buf][:, at + a:at + (w if b is None else b):step], [name] if key is None else [key] if isinstance(key, str) else list(key)

    def ix(win, off):
        return win[0].indirect(off[0]), win[1] + off[1]

    def cast(x, d):
        return x[0].bitcast(d), x[1]

    def op(q, fn, outs, ins):
        R = sorted({k for o in ins for k in o[1]})
        W = sorted({k for o in outs for k in o[1]} | {k for k in R if k in PSUM})
        deps(q, R, W)
        total[own[q]] = total.get(own[q], 0) + 1
        fn().then_inc(T.sem[own[q]], 1)
        note(own[q], q, R, W)

    def dma(q, pairs, sem, R, W):
        deps(q, R, W)
        for o, i in pairs:
            queue[q].dma_start(o, i).then_inc(T.sem[sem], 16)
            total[sem] = total.get(sem, 0) + 16
        note(sem, q, R, W)

    v, s = g.vector, g.scalar

    def val(x):
        return x[0] if isinstance(x, tuple) else x

    def ts(out, in0, a, o0, b=None, o1=None):
        ins = [in0] + [x for x in (a, b) if isinstance(x, tuple)]
        if o1 is None:
            op("v", lambda: v.tensor_scalar(out[0], in0[0], val(a), None, o0), [out], ins)
        else:
            op("v", lambda: v.tensor_scalar(out[0], in0[0], val(a), val(b), o0, o1), [out], ins)

    def tt(out, a, b, o):
        op("v", lambda: v.tensor_tensor(out[0], a[0], b[0], o), [out], [a, b])

    def cp(out, in_):
        op("v", lambda: v.tensor_copy(out[0], in_[0]), [out], [in_])

    def fill(out, c):
        op("v", lambda: v.memset(out[0], c), [out], [])

    def scan(out, d0, d1, init, o0, o1):
        op("v", lambda: v.tensor_tensor_scan(out[0], d0[0], d1[0], val(init), o0, o1), [out], [d0, d1] + ([init] if isinstance(init, tuple) else []))

    def turn(out, in_):
        op("v", lambda: v.transpose(out[0], in_[0]), [out], [in_])

    def act(out, in_, func=F.Copy, **kw):
        op("s", lambda: s.activation(out[0], in_[0], func, **kw), [out], [in_])

    def sfill(out, n, c):
        if c:
            act(out, p("nr24", 0, n), F.Identity, scale=0.0, bias=c)
        else:
            act(out, p("nr24", 0, n), scale=0.0)

    def signs(junk, in_, bias, accum):
        op("s", lambda: s.activation(junk[0], in_[0], F.Sign, bias=bias[0], accum_out=accum[0], scale=-1.0), [junk, accum], [in_, bias])

    def copy(q, out, in_):
        (cp if q == "v" else act)(out, in_)

    def gcopy(out, in_, n):
        op("g", lambda: g.affine_select(out[0], in_[0], [[0, n]], A.is_equal, 0.0, 0, 0), [out], [in_])

    def scaled(q, out, in_, c):
        if q == "s":
            act(out, in_, scale=c)
        else:
            ts(out, in_, c, A.mult)

    def quant(c, sc, in_):
        op("v", lambda: v.quantize_mx(c[0], sc[0], in_[0]), [c, sc], [in_])

    def mm(out, l, ls, r, rs):
        op("t", lambda: g.tensor.matmul_mx(out[0], l[0], ls[0], r[0], rs[0], True, True), [out], [l, ls, r, rs])

    def iota(out, pattern, base=0, ch=0):
        op("g", lambda: g.iota(out[0], pattern, base, ch, allow_small_or_imprecise_dtypes=True), [out], [])

    def lane_scan(out, row, n):
        scan(out, p("D2", 0, n), row, 0.0, A.mult, A.max)

    def unlane(out, rows, off=0.0):
        ts(out, rows, p("pw", 15, 16), A.mult, -2048.0 - off, A.add)

    def XT(t, b=None, h=None):
        if b is not None:
            return p("XT%d" % t, b, 4 * C, 4, ["XT%d_%d%d" % (t, b, i) for i in range(2)])
        return p("XT%d" % t, 4 * H * h, 4 * H * h + 4 * H, 1, ["XT%d_%d%d" % (t, i, h) for i in range(4)])

    def xq(t, h=None):
        a, e, hs = (0, C, (0, 1)) if h is None else (H * h, H * h + H, (h,))
        return [p("%s%d" % (n, t), a, e, 1, ["%s%d_%d" % (n, t, i) for i in hs]) for n in ("xq", "xs")]

    def WB(b, a, e, parts):
        return p("WB", WEND * b + a, WEND * b + e, 1, ["W%s_%d" % (k, b) for k in parts])

    BANK = ("psa", "psb")

    def quant_x(t, h):
        quant(*xq(t, h), XT(t, None, h))

    def planes(t, q, bs):
        for b in bs:
            if q == "g":
                gcopy(WB(b, 0, C, "X"), XT(t, b), C)
            else:
                copy(q, WB(b, 0, C, "X"), XT(t, b))

    def scores(t, h):
        mm(p(BANK[h], 0, H), p("ur", 0, 128), p("urs", 0, 128), *xq(t, h))

    def scores_late(t):
        mm(p("psl", 0, C), p("ur", 128, 256), p("urs", 128, 256), *xq(t))

    def rise(t, h):
        o = p("P0", 4 * H * h + 1, 4 * H * h + 4 * H, 4, "P0r%d" % h)
        if t == 0:
            ts(o, p(BANK[h], 0, H), 0.0, A.is_gt)
        else:
            tt(o, p(BANK[h], 0, H), p("LAST", H * h, H * h + H, 1, "LAST%d" % h), A.is_gt)

    FLAGS = ["P0", "P0r0", "P0r1", "P0v"]

    def entries(beside=(lambda: None,) * 3):
        flags, y = p("P0", 1, 4 * CV, 4, FLAGS), p("P1", 0, 4 * CV, 4, "P1y")
        zeros = p("P1", 1, 4 * CV, 4, "P11")
        scan(y, flags, zeros, -161.0, A.add, A.min)
        signs(p("junk1"), y, p("thr"), p("ac1"))
        beside[0]()
        scan(p("RQ", 1, CV + 1), flags, zeros, p("vini"), A.add, A.add)
        beside[1]()
        scan(p("DQ"), p("RQ", 1, CV + 1), p("RQ", 0, CV, 1, ["RQ", "RQ0"]), 0.0, A.max, A.subtract)
        beside[2]()
        scan(p("ST", 0, CV), p("DQ"), p("I32"), -8.0, A.add, A.min)

    def runs_end(t):
        ts(p("al"), p("ac1"), float(CV), A.add, 0.5, A.mult)
        ts(p("el%d" % t), ix(p("ST", key=["ST", "STz"]), p("al")), 32.0, A.mult, 200.0, A.add)
        send_list(p("el%d" % t, 0, LT), T["rt%d" % t][:, 0:LT], "rb%d" % t)

    def late():
        o = p("P0", 2, 4 * C, 4, "P0l")
        op("s", lambda: s.activation(o[0], p("psl", 0, C)[0], F.Sign, bias=-2.0 ** -118), [o], [p("psl")])

    def signed():
        scan(p("Z", 0, NZ), p("P0", 0, NZ, 1, FLAGS + ["P0l", "P0m", "P0z"]), p("P1", 0, NZ, 1, ["P1y", "P11", "P12", "P13"]), 0.0, A.mult, A.add)

    ends = p("rk", 24, 26, 1, "endl")

    def resolve(t):
        act(p("ZS", 224, CS, 1, "ZSb"), ix(p("Z", 0, NZ), p("pib")))
        cp(p("ZS", 0, 224, 1, "ZSa"), ix(p("Z", 0, NZ), p("pia")))
        if t:
            older_halves(t, (2, 3))
        else:
            act(p("tgx", 0, C), ix(p("xio", 0, C), p("tgp")), F.Identity, scale=0.25, bias=2048.0 - 2051.0 / 4)
        zs = p("ZS", key=["ZSa", "ZSb"])
        scan(p("SD1", 1, CS + 1), p("NS"), zs, 0.0, A.mult, A.max)
        cp(p("wm%d" % t, 0, 32, 1, "wm%da" % t), ix(p("SD1", 0, CS, 1, ["SD1", "SD10"]), ends))
        send_list(p("wm%d" % t, 0, 24, 1, "wm%da" % t), T["rw%d" % t][:, 0:24], "rl%d" % t)
        if t < 2:
            scan(p("SD2", 1, CS + 1), p("NS"), zs, 0.0, A.mult, A.min)
            act(p("wm%d" % t, 32, 64, 1, "wm%db" % t), ix(p("SD2", 0, CS, 1, ["SD2", "SD20"]), ends), scale=-1.0)
            send_list(p("wm%d" % t, 32, 56, 1, "wm%db" % t), T["rw%d" % t][:, 32:56], "rm%d" % t)

    def gather_e(t, pairs):
        for b, q in pairs:
            copy(q, p("ET", b, None, 4, "ET%d" % b), ix(WB(b, 0, M1, "X0"), p("el%d" % t, 0, LT)))

    def quant_e(t):
        quant(p("eq%d" % t), p("xs%d" % t, C, C + K, 1, "es%d" % t), p("ET", 0, None, 1, ["ET%d" % b for b in range(4)]))
        send_codes(t)

    rel = _relays(rank, T, topo)

    def send(i, out, in_, sem):
        rid, pid = topo.addr(rel[i], core)
        g.remote_dma(out, in_, T.sem[sem], T.sem.ls, pid, rid, topo.mask(core, rel[i]))
        total["ls"] = total.get("ls", 0) + len(topo.engines(core, rel[i]))

    def share(srcs, dsts, sem):
        es = topo.engines(core, rel[0])
        h, tr = len(es) // len(srcs), []
        for i, (src, dst) in enumerate(zip(srcs, dsts)):
            rid, pid = topo.addr(rel[i], core)
            tr.append(RemoteDMATransfer(dst_ids=[DstId(rid=rid, pnc=pid)], dma_engine_mask=_bits(es[h * i:h * i + h]), remote_sem=T.sem[sem], src=src, dst=dst))
        g.remote_dma_fused(tr, local_sem=T.sem.ls)
        total["ls"] = total.get("ls", 0) + len(es)

    def send_codes(t):
        deps("g", ["eq%d" % t, "es%d" % t, "xs%d_1" % t], [])
        ends = [min(THIRD * i + THIRD, K) for i in range(3)]
        share([T["eq%d" % t][:, e - THIRD:e].bitcast(dt.uint8) for e in ends] + [T["xs%d" % t][:, C + K - 4 * THIRD:C + K]],
              [T["rc%d" % t][:, 0:THIRD].bitcast(dt.uint8)] * 3 + [T["rs%d" % t][:, 0:4 * THIRD]], "rh%d" % t)

    def send_list(src, dst, sem):
        deps("g", src[1], [])
        send(3, dst, src[0], sem)

    def unpack(t):
        for b in range(4):
            mm(p("pw%d" % b, 0, K), p("ebq%d" % b), p("ebs%d" % b), p("hq%d" % t), p("hs%d" % t))

    def fired():
        scan(p("FS"), p("DA"), p("Z", 1, 4 * C, 4), 0.0, A.add, A.min)

    def ends_of(t):
        op("s", lambda: s.activation(p("sg")[0], p("FS", 15, C, 16)[0], F.Sign, bias=p("thr2")[0]), [p("sg")], [p("FS"), p("thr2")])
        act(p("F1", 0, 96, 4, "F1d"), p("sg"), F.Identity, scale=80.0, bias=-80.0 - V1 - 320 * t)
        if t >= 1:
            act(p("G1s", 0, 72, 3, "G1d"), p("sg"), F.Identity, scale=80.0, bias=-80.0 - V1 - 320 * (t - 1))

    def older_winners(t):
        was = p("lw%d" % (t - 1), 32, 56, 1, "lx%d" % (t - 1))
        act(p("G0s", 1, 72, 3, "G0w"), was)
        act(p("G0s", 2, 72, 3, "G0n"), was, F.Relu, scale=-BIG, bias=BIG)
        act(p("F0", 2, 96, 4, "F0o"), was, scale=BIG)

    def older_places():
        scan(p("GQ"), p("G0s", key=["FG", "G0w", "G0n"]), p("G1s", key=["FG", "G1d", "G1c"]), 0.0, A.add, A.min)
        act(p("F1", 3, 96, 4, "F1r"), p("GQ", 2, 72, 3))

    def last(hs):
        for h in hs:
            act(p("LAST", H * h, H * h + H, 1, "LAST%d" % h), p(BANK[h], 0, H))

    def older_halves(t, bs):
        for b in bs:
            act(p("XD%d" % b), ix(WB(b, 0, M1, ["X", "0"]), p("lt%d" % (t - 1))), scale=0.5)

    def older_means(t):
        for b in range(4):
            tt(WB(b, V1 + 320 * (t - 1), V1 + 320 * (t - 1) + K, ["A%d" % (t - 1)]), p("pw%d" % b, 0, K), p("XD%d" % b), A.add)

    def targets(t):
        act(p("TT"), ix(p("tgx", key=["tgx", "tgxp"]), p("le%d" % t)))
        lane_scan(p("TS"), p("TT"), K)
        unlane(p("lt%d" % t), p("TS", 15, K, 16))

    def halves(t, pairs):
        for b, q in pairs:
            scaled(q, p("XG%d" % b), ix(WB(b, 0, M1, ["X", "0"]), p("lt%d" % t)), 0.5)

    def merge(n):
        t = n - 1
        lw, m, a = p("lw%d" % t, 0, 24), M1 + 320 * t, V1 + 320 * t
        for b in range(4):
            mm(p("pw%d" % b, 0, K), p("wl", 128 * b, 128 * b + 128), p("wls", 128 * b, 128 * b + 128), p("ql%d" % t), p("qls%d" % t))
        for b, q in ((0, "v"), (1, "s"), (2, "v"), (3, "s")):
            o, i = p("HT", b, None, 4, "HT%d" % b), p("pw%d" % b, 0, K)
            if q == "s":
                act(o, i, F.Relu, scale=0.03125)
            else:
                ts(o, i, 0.0, A.max, 0.03125, A.mult)
        quant(p("hq%d" % t), p("hs%d" % t), p("HT", 0, None, 1, ["HT%d" % b for b in range(4)]))
        unpack(t)
        if n == 1:
            ends_of(0)

        def winners():
            act(p("F0", 1, 96, 4, "F0w"), lw)
            act(p("F0", 3, 96, 4, "F0n"), lw, F.Relu, scale=-BIG, bias=BIG)

        def places():
            scan(p("FQ"), p("F0", key=["FG", "F0w", "F0o", "F0n"]), p("F1", key=["FG", "F1d", "F1r"]), 0.0, A.add, A.min)

        def table():
            ts(p("fin"), p("FQ", 3, 96, 4), -1.0, A.mult)

        def mean(b):
            tt(WB(b, a, a + K, ["A%d" % t]), p("pw%d" % b, 0, K), p("XG%d" % b), A.add)

        def move(b):
            act(WB(b, m, m + K, ["M%d" % t]), p("pw%d" % b, 0, K), scale=2.0)

        if n == 1:
            mean(0), move(1), mean(2), move(3), winners(), mean(1), move(0), mean(3), places(), move(2), table()
        else:
            winners(), mean(0), move(1), mean(2), places(), move(3), mean(1), table(), move(0), mean(3), move(2)
        for b, q in ((0, "s"), (1, "v"), (2, "s"), (3, "v")):
            copy(q, XT(n, b), ix(WB(b, 0, a + K, ["X", "0"] + ["%s%d" % (k, i) for i in range(n) for k in "MA"]), p("fin")))

    arrivals = [("lg", 8, ["tgp"]), ("lq", 64, ["wl", "wls"])]
    for t in range(3):
        arrivals += [("lb%d" % t, 8, ["le%d" % t]), ("la%d" % t, 8, ["lw%d" % t]), ("ha%d" % t, 32, ["ql%d" % t, "qls%d" % t])]
        arrivals += [("lm%d" % t, 8, ["lx%d" % t])] if t < 2 else []
    for sem, n, keys in arrivals:
        total[sem] = n
        note(sem, None, [], keys)

    dma("s", [(T.tgT[:, :], T.tg[:, :])], "dtg", [], ["tgT"])
    dma("y", [(T.UT[:, :], T.u[:, :])], "du", [], ["UT"])
    dma("s", [(T.XT0[:, 0:4 * H], T.x[:, 0:4 * H])], "dxa", [], XT(0, None, 0)[1])
    dma("y", [(T.XT0[:, 4 * H:4 * C], T.x[:, 4 * H:4 * C])], "dxb", [], XT(0, None, 1)[1])

    fill(p("nr24"), 1.0)
    nr24, ones32 = p("nr24", 0, 576), p("nr24", 576, 608)
    iota(p("lanep"), [[1, 1]], 0, 1)
    iota(p("x36"), [[16, 36]])
    iota(p("r48"), [[0, 12], [16, 3]])
    iota(p("KC"), [[1, 24], [0, 24]])
    dma("y", [(T.wsp[:, :], T.ws[:, :])], "dws", [], ["wsp"])
    dma("y", [(T.wq[:, :].bitcast(dt.uint8), T.wc[:, :])], "dwc", [], ["wq"])

    def affine(out, in_, a, b):
        act(out, in_, F.Identity, scale=a, bias=b)

    ts(p("lanei"), p("lanep"), 15, A.bitwise_and)
    fill(p("nr24", 0, 576, 24), 0.0)
    cp(p("lane"), p("lanei"))
    cp(p("lu", 0, 8), p("x36", 0, 8))
    ts(p("xf"), p("x36"), p("lane"), A.add)
    ts(p("lu", 8, 16, 1, "ll"), p("x36", 0, 8), 1.0, A.add)
    ts(p("RL"), p("r48"), p("lane"), A.add)
    ts(p("own"), p("x36", 0, 16), 1.0 / 16, A.mult, p("lane"), A.is_equal)
    ts(p("l26"), p("x36", 0, 26), 0.0, A.mult, p("lane"), A.add)
    fill(p("nx2", 0, 1, 1, "nx0"), 0.0)
    ts(p("nx2", 1, 16), p("own", 0, 15), -255.0 / 1024, A.mult)
    ts(p("nxf"), p("xf", 0, 24), -1.0, A.mult)
    sfill(p("Hh"), 32, 0.0)
    sfill(p("hlf"), 16, 0.5)
    sfill(p("nr16"), 32, 1.0)
    affine(p("q1"), p("xf"), 1.0 / 24, -11.5 / 24)
    sfill(p("nr16", 0, 32, 16), 2, 0.0)
    affine(p("q3"), p("xf"), -24.0, 552.0)
    ts(p("fl"), p("q1"), R1, A.add, R1, A.subtract)
    scan(p("pw"), p("hlf"), p("own"), 0.0, A.mult, A.max)
    tt(p("PA"), p("nx2", key=["nx2", "nx0"]), p("own"), A.add)
    ts(p("thr2"), p("own", 15, 16), -255.0, A.mult, 255.5, A.add)
    affine(p("q4"), p("fl"), 577.0, 0.0)
    act(p("D2"), ix(p("own"), p("l26")), F.Identity, scale=-2.0, bias=2.0)
    affine(p("vini"), p("lane"), -1.0, 2064.0 + 7.5)
    affine(p("thr"), p("lane"), 16.0, -145.5)
    sfill(p("BI", 0, 1, 1, "BI0"), 1, -1.0 - MID)
    sfill(p("P0", 0, NZ, 4, "P0"), C + 1, 0.0)
    sfill(p("P0", 4 * C + 2, 4 * C + 4, 1, "P0z"), 2, 0.0)
    sfill(p("P0", 4 * C + 1, 4 * CV, 4, "P0v"), 16, 1.0)
    sfill(p("RQ", 0, 1, 1, "RQ0"), 1, 2064.0)
    sfill(p("ST", CV, CV + 1, 1, "STz"), 1, (C - 200) / 32.0)
    sfill(p("WB", C, None, WEND, ["W0_%d" % b for b in range(4)]), 4, 0.0)
    tt(p("q6"), p("q4"), p("q3"), A.add)
    sfill(p("P1", 1, 4 * CV, 4, "P11"), CV, 0.0)

    for a in range(2):
        ts(p("vi", 24 * a, 24 * a + 24, 1, "vi%d" % a), p("tgT"), 4, A.arith_shift_right)
    cp(p("tgu"), p("tgT"))
    cp(p("PL"), p("q6"))
    send_list(p("tgu"), T.rtg[:, 0:24], "rg")
    iota(p("xio", 0, C), [[4, C]], 2048 + 3)
    iota(p("xio", C, CS, 1, "xioz"), [[0, CS - C]], 2048 + NZ - 1)
    XIO = ["xio", "xioz"]
    iota(p("P1", 2, NZ, 4, "P12"), [[0, C + 1]])
    planes(0, "g", (0,))
    deps("g", ["wsp"], [])
    share([T.wsp[:, 128 * i:128 * i + 128] for i in range(4)], [T.rws[:, 0:128]] * 4, "rp")
    deps("g", ["wq"], [])
    share([T.wq[:, 128 * i:128 * i + 128].bitcast(dt.uint8) for i in range(4)], [T.rwq[:, 0:128].bitcast(dt.uint8)] * 4, "rq")
    planes(0, "g", (1, 2))
    tt(p("OH"), ix(p("vi", key=["vi0", "vi1"]), p("RL")), p("KC"), A.is_equal)
    quant(p("uq"), p("us"), p("UT"))
    scan(p("C1"), nr24, p("OH"), 0.0, A.mult, A.add)
    lu = p("lu", key=["lu", "ll"])
    act(p("urs"), ix(p("us"), lu))
    act(p("NOm"), ix(p("OH"), p("PL")), scale=-1000.0)
    cp(p("Hh", 0, 24), p("C1", 23, 576, 24))
    cp(cast(p("ur"), dt.uint32), ix(cast(p("uq"), dt.uint32), lu))
    turn(p("HT1"), p("Hh"))
    quant_x(0, 0)
    scores(0, 0)
    scan(p("PI"), p("nr16"), p("HT1"), 0.0, A.mult, A.add)
    quant_x(0, 1)
    scores(0, 1)
    tt(p("G1", 0, 32), p("PI"), p("HT1"), A.subtract)
    for a in range(2):
        ts(p("G1", 32 + 16 * a, 48 + 16 * a, 1, "G1%d" % a), p("nr24", 576, 592), p("PI", 16 * a + 15, 16 * a + 16), A.mult, 1.0, A.add)
    rise(0, 0)
    turn(p("GT"), p("G1", key=["G1", "G10", "G11"]))
    rise(0, 1)
    scan(p("BI", 1, 33), ones32, p("GT", 32, 64), -1.0 - MID, A.mult, A.add)
    act(p("I32"), p("xio", 0, CV, 1, XIO), F.Identity, scale=1.0 / 128, bias=-2851.0 / 128)
    scores_late(0)
    late()
    tt(p("G2"), p("GT", 0, 24), p("BI", 0, 24, 1, ["BI", "BI0"]), A.add)
    entries((lambda: tt(p("OH", 0, 576, 24), p("OH", 0, 576, 24), p("G2"), A.add),
             lambda: scan(p("C2"), nr24, p("OH"), 0.0, A.mult, A.add),
             lambda: None))
    act(p("C2m"), ix(p("C2"), p("PL")))
    ts(p("bx"), p("BI", 1, 33), 2048.0 + 1 + MID, A.add)
    planes(0, "s", (3,))
    runs_end(0)
    lane_scan(p("be"), p("bx"), 32)
    unlane(ends, p("be", 15, 32, 16), 1.0)
    iota(p("P1", 3, NZ, 4, "P13"), [[0, C + 1]])
    op("g", lambda: g.affine_select(T.EBW[:, :], p("nr24", 0, 516)[0], [[1, 516]], A.is_equal, 0.0, -3, -4), [p("EBW")], [p("nr24")])
    scan(p("SEL"), p("NOm"), p("C2m"), -2000.0, A.add, A.max)
    ts(p("rk", 0, 24), p("SEL", 23, 576, 24), float(MID), A.add)
    gather_e(0, ((0, "s"), (1, "s"), (2, "s"), (3, "s")))
    act(p("P0", 3, 4 * C, 4, "P0m"), ix(p("D2", 0, C), p("tgu")), F.Identity, scale=-0.5, bias=1.0)
    cp(ix(p("pir"), p("rk", key=["rk", "endl"])), p("xio", key=XIO))
    act(p("NS"), p("pir"), F.Sign, scale=-1.0, bias=2048.0 + NZ - 1)
    quant_e(0)
    iota(p("F0", 0, 4 * 96, 1, "FG"), [[0, 4 * 96]], int(BIG))
    iota(p("F0", 2, 96, 4, ["F0o", "FG"]), [[0, 24]])
    for o in (p("F1", 3, 96, 4, ["F1r", "FG"]), p("G1s", 2, 72, 3, ["G1c", "FG"])):
        gcopy(o, p("nxf"), 24)
    iota(p("tgx", C, C + 1, 1, "tgxp"), [[1, 1]], 2048)
    lane_scan(p("pis"), p("pir"), CS)
    unlane(p("pib"), p("pis", 239, CS, 16))
    unlane(p("pia"), p("pis", 15, 224, 16))
    sfill(p("SD1", 0, 1, 1, "SD10"), 1, 0.0)
    act(p("EBW"), p("EBW"), scale=0.5)
    signed()
    sfill(p("SD2", 0, 1, 1, "SD20"), 1, 0.0)
    resolve(0)
    dma("y", [(T.VT[:, :], T.v[:, :])], "dv", ["wm0b"], ["VT"])
    for b in range(4):
        quant(p("ebq%d" % b), p("ebs%d" % b), p("EBW", 3 - b, 515 - b))
    targets(0)
    act(p("DA"), ix(p("PA"), p("l26", 0, 24)), scale=1024.0)
    halves(0, ((0, "v"), (1, "s"), (2, "v"), (3, "s")))
    fired()
    iota(p("iotaj", 0, C), [[1, C]])
    iota(p("iotaj", C, C + 1, 1, "iotajp"), [[1, 1]], -1)

    for t in (1, 2):
        merge(t)
        if t == 1:
            last((0, 1))
        planes(t, "g", (0, 1, 2))
        planes(t, "s", (3,))
        for h in range(2):
            quant_x(t, h)
            scores(t, h)
        scores_late(t)
        rise(t, 0)
        rise(t, 1)
        entries()
        late()
        runs_end(t)
        gather_e(t, ((3, "s"), (0, "v"), (2, "s"), (1, "v")))
        quant_e(t)
        if t == 1:
            last((0, 1))
        unpack(t - 1)
        older_halves(t, (0, 1))
        signed()
        resolve(t)
        fired()
        ends_of(t)
        older_means(t)
        targets(t)
        older_winners(t)
        older_places()
        halves(t, ((0, "v"), (1, "s"), (2, "v"), (3, "s")))
    quant(p("vq"), p("vs"), p("VT"))

    merge(3)
    act(p("OLr"), ix(p("iotaj", key=["iotaj", "iotajp"]), p("el2", 0, LT)))
    dma("y", [(T.ol[:, :], T.OLr[0:128:16, :])], "dol", ["OLr"], [])
    for h in range(2):
        a, e = H * h, H * h + H
        quant_x(3, h)
        mm(p(BANK[h], 0, H), p("vq"), p("vs"), *xq(3, h))
        dma("y", [(T.oc[:, 4 * a:4 * e], T.xq3[:, a:e].bitcast(dt.uint8))], "doc%d" % h, ["xq3_%d" % h], [])
    act(p("YT", 0, H, 1, "YT0"), p("psa", 0, H))
    cp(p("YT", H, C, 1, "YT1"), p("psb", 0, H))
    dma("s", [(T.y[:, 0:H], T.YT[:, 0:H])], "dy0", ["YT0"], [])
    dma("y", [(T.osc[4 * k:4 * k + 4, :], T.xs3[32 * k:32 * k + 4, 0:C]) for k in range(4)], "dos", ["xs3_0", "xs3_1"], [])
    dma("s", [(T.y[:, H:C], T.YT[:, H:C])], "dy1", ["YT1"], [])
    for sem in sorted(total):
        if waited.get(sem, 0) < total[sem]:
            g.wait_ge(T.sem[sem], total[sem])
